import numpy as np
import ml_dtypes


def mxq(x, axis, fmt="e4m3"):
    dtype, down = {"e4m3": (ml_dtypes.float8_e4m3fn, 7), "e5m2": (ml_dtypes.float8_e5m2, 14)}[fmt]
    v = np.moveaxis(np.asarray(x, np.float32).astype(ml_dtypes.bfloat16).astype(np.float64), axis, -1)
    blocks = v.reshape(v.shape[:-1] + (-1, 32))
    amax = np.abs(blocks).max(-1, keepdims=True)
    byte = np.maximum(np.where(amax > 0, np.frexp(amax)[1] - 1 + 127, 0) - down, 1)
    scale = np.exp2(byte - 127.0)
    codes = (blocks / scale).astype(np.float32).astype(dtype).astype(np.float64)
    return np.moveaxis((codes * scale).reshape(v.shape), -1, axis)


WIDE = False


def mx_kscale(k):
    if not WIDE:
        return np.ones(k)
    levels = np.array([10, -10, 5, -5, 0])
    if k % 512:
        return np.exp2(np.random.permutation(np.resize(levels, k // 32))).repeat(32)
    a = np.empty((k // 512, 16))
    for p in range(k // 512):
        a[p, :8] = np.random.permutation(np.resize(levels, 8))
        for g in range(8):
            far = levels[np.abs(levels - a[p, g]) >= 10]
            a[p, g + 8] = far[np.random.randint(len(far))]
    return np.exp2(a.ravel()).repeat(32)


def f64(x):
    return np.asarray(x).astype(np.float64)


def striped(idx):
    return np.tile(idx.reshape(-1, 16).T, (8, 1)).astype(np.uint16)


def unstriped(offs):
    return offs[:16].T.reshape(-1).astype(np.int64)


E2M1 = np.array([0.0, 0.5, 1.0, 1.5, 2.0, 3.0, 4.0, 6.0, -0.0, -0.5, -1.0, -1.5, -2.0, -3.0, -4.0, -6.0])


def pack_weight(w, fmt):
    k, n = w.shape
    w = f64(np.asarray(w, np.float32).astype(ml_dtypes.bfloat16)).reshape(k // 32, 32, n)
    amax = np.abs(w).max(1)
    if fmt == "e4m3":
        byte = np.frexp(amax)[1] - 1 + 127 - 7
    else:
        mant, ex = np.frexp(amax / 6.0)
        byte = np.where(mant > 0.5, ex, ex - 1) + 127
    byte = np.clip(np.where(amax > 0, byte, 1), 1, 254)
    scaled = (w * np.exp2(127.0 - byte)[:, None, :]).reshape(k, n).astype(np.float32)
    by_word = np.ascontiguousarray(scaled.reshape(k // 512, 128, 4, n).transpose(0, 1, 3, 2))
    if fmt == "e4m3":
        words = by_word.astype(ml_dtypes.float8_e4m3fn).view(np.uint8)
    else:
        c = by_word.astype(ml_dtypes.float4_e2m1fn).view(np.uint8) & 0xF
        words = (c[..., 0::2] | (c[..., 1::2] << 4)).reshape(k // 512, 128, 2 * n)
    return np.ascontiguousarray(words), np.ascontiguousarray(byte.astype(np.uint8).reshape(k // 512, 16, n))


def unpack_weight(words, scales, fmt):
    g, _, n = scales.shape
    words = np.ascontiguousarray(words).reshape(g, 128, n, -1)
    if fmt == "e4m3":
        vals = words.view(ml_dtypes.float8_e4m3fn).astype(np.float64)
    else:
        nib = np.empty((g, 128, n, 4), np.uint8)
        nib[..., 0::2] = words & 0xF
        nib[..., 1::2] = words >> 4
        vals = E2M1[nib]
    vals = vals * np.repeat(np.exp2(scales.astype(np.float64) - 127.0), 8, axis=1)[..., None]
    return vals.transpose(0, 1, 3, 2).reshape(g * 512, n)


def gelu(v):
    return 0.5 * v * (1.0 + np.tanh(np.sqrt(2.0 / np.pi) * (v + 0.044715 * v**3)))


def bf(x):
    return np.asarray(x, np.float32).astype(ml_dtypes.bfloat16)


def planes(Y):
    n, m = Y.shape
    b = f64(bf(Y)).reshape(n // 32, 32, m)
    amax = np.abs(b).max(1)
    byte = np.clip(np.where(amax > 0, np.frexp(amax)[1] - 1 + 127 - 7, 1), 1, 254)
    codes = (b * np.exp2(127.0 - byte)[:, None, :]).reshape(n, m).astype(np.float32).astype(ml_dtypes.float8_e4m3fn).view(np.uint8)
    words = codes.reshape(n // 512, 128, 4, m).transpose(0, 1, 3, 2)
    return np.ascontiguousarray(words), np.ascontiguousarray(byte.astype(np.uint8).reshape(n // 512, 16, m))


K, T, S, H, N = 1024, 4096, 1024, 512, 768

def setup_inputs():
    n = np.random.standard_normal
    s = mx_kscale(K)[:, None]
    u = mx_kscale(H)[:, None]
    tab_words, tab_scales = pack_weight(n((K, T)) * s, "e4m3")
    w2_words, w2_scales = pack_weight(1.5 * n((K, H)) / np.sqrt(K) / s * u.T, "e2m1")
    w3_words, w3_scales = pack_weight(1.5 * n((H, N)) / np.sqrt(H) / u, "e4m3")
    return {
        "tab_words": tab_words, "tab_scales": tab_scales,
        "offs": striped(np.random.permutation(T)[:S]),
        "w1": (n((K, H)) / np.sqrt(K) / s).astype(np.float32),
        "w2_words": w2_words, "w2_scales": w2_scales,
        "w3_words": w3_words, "w3_scales": w3_scales,
        "centres": n(H).astype(np.float32),
        "least": (0.7 * n((N, S))).astype(np.float32),
    }

def reference(tab_words, tab_scales, offs, w1, w2_words, w2_scales,
              w3_words, w3_scales, centres, least):
    v = unpack_weight(tab_words, tab_scales, "e4m3")[:, unstriped(offs)]
    a = mxq(f64(w1), 0, "e4m3").T @ v
    b = unpack_weight(w2_words, w2_scales, "e2m1").T @ v
    gap = a - f64(centres)[:, None]
    h = 1.0 / (1.0 + gap * gap) * b
    hq = mxq(h, 0, "e4m3")
    match = unpack_weight(w3_words, w3_scales, "e4m3").T @ hq
    y = np.maximum(match, f64(least))
    words, scales = planes(h)
    return y, h, words, scales

@@ -1,0 +1,287 @@
+from contextlib import ExitStack
+
+import concourse.mybir as mybir
+
+K, T, S, H, N = 1024, 4096, 1024, 512, 768
+FLOPS = 2 * (2 * K * H * S + H * N * S)
+
+F32 = mybir.dt.float32
+BF16 = mybir.dt.bfloat16
+I32 = mybir.dt.int32
+U32 = mybir.dt.uint32
+U16 = mybir.dt.uint16
+U8 = mybir.dt.uint8
+E4M3 = mybir.dt.float8_e4m3fn_x4
+E2M1 = mybir.dt.float4_e2m1fn_x4
+ACT = mybir.ActivationFunctionType
+ALU = mybir.AluOpType
+
+P = 128
+PACK = 4
+PASSES = K // (P * PACK)
+QUADS = 4
+SLICE = 512
+CHUNKS = [(0, 256), (256, 512), (512, 768), (768, 896), (896, 1024)]
+H_STORES = CHUNKS
+Y_STORES = CHUNKS
+CODE_STORES = [(0, 512), (512, 1024)]
+ACT_ROUND = (2, 3)
+DVE_SQUARE = (0,)
+PAIRS = N // (2 * P)
+
+
+def holder(spans, col):
+    for span in spans:
+        if span[0] <= col < span[1]:
+            return span
+    raise ValueError(col)
+
+
+def tile_list_lidar_radar_resonance_kernel(
+    tc, tab_words, tab_scales, offs, w1, w2_words, w2_scales, w3_words, w3_scales, centres, least,
+    out_0, out_1, out_2, out_3,
+):
+    nc = tc.nc
+    with ExitStack() as ctx:
+        keep = ctx.enter_context(tc.tile_pool(name="keep", bufs=1))
+        work = ctx.enter_context(tc.tile_pool(name="work", bufs=2))
+        psum = ctx.enter_context(tc.psum_pool(name="psum", bufs=1))
+
+        offsets = keep.tile([P, S // 16], U16, name="offsets")
+        tab_rows = keep.tile([P, T], U8, name="tab_rows", align_bytes=64)
+        w2_plane_raw = keep.tile([P, PASSES, H], U8, name="w2_plane_raw", align_bytes=64)
+        w3_plane = keep.tile([P, N], U8, name="w3_plane", align_bytes=64)
+        v_plane = [keep.tile([P, S], U8, name=f"v_plane{a}", align_bytes=64) for a in range(PASSES)]
+        one = keep.tile([P, 1], F32, name="one")
+        warm = keep.tile([P, 1], F32, name="warm")
+
+        nc.vector.memset(tab_rows[:].bitcast(I32), 0)
+        nc.vector.memset(w2_plane_raw[:].rearrange("p a c -> p (a c)").bitcast(I32), 0)
+        nc.vector.memset(one[:], 1.0)
+        nc.vector.memset(w3_plane[:].bitcast(I32), 0)
+        for a in range(PASSES):
+            nc.vector.memset(v_plane[a][:].bitcast(I32), 0)
+        nc.scalar.activation(warm[:], one[:], ACT.Abs_reciprocal_sqrt)
+
+        w1_raw = [keep.tile([P, PACK, H], F32, name=f"w1_raw{a}") for a in range(PASSES)]
+        tab = [keep.tile([P, T], U32, name=f"tab{a}", align_bytes=64) for a in range(PASSES)]
+        w2_raw = keep.tile([P, PASSES, 2 * H], U8, name="w2_raw", align_bytes=64)
+        w3_codes = keep.tile([P, N], U32, name="w3_codes", align_bytes=64)
+        centre = keep.tile([P, PACK], F32, name="centre")
+        floor = [keep.tile([P, 2, S], F32, name=f"floor{i}") for i in range(PAIRS)]
+
+        def load_w1(a):
+            nc.sync.dma_start(w1_raw[a][:], w1[512 * a : 512 * (a + 1), :].rearrange("(p j) c -> p j c", j=PACK))
+
+        nc.sync.dma_start(offsets[:], offs)
+        load_w1(0)
+        nc.sync.dma_start(
+            tab_rows[0:P:4, :].bitcast(I32), tab_scales.rearrange("a q t -> (a q) t").bitcast(I32)
+        )
+        nc.sync.dma_start(w2_raw[:].bitcast(I32), w2_words.rearrange("a p b -> p a b").bitcast(I32))
+        for q in range(QUADS):
+            nc.sync.dma_start(
+                w2_plane_raw[32 * q : 32 * q + 4, :, :].bitcast(I32),
+                w2_scales[:, 4 * q : 4 * q + 4, :].rearrange("a r c -> r a c").bitcast(I32),
+            )
+        load_w1(1)
+        for a in range(PASSES):
+            nc.sync.dma_start(tab[a][:].bitcast(I32), tab_words[a].rearrange("p t i -> p (t i)").bitcast(I32))
+        nc.sync.dma_start(centre[:], centres.rearrange("(p t) -> p t", t=PACK))
+        nc.sync.dma_start(w3_codes[:].bitcast(I32), w3_words[0].rearrange("p c i -> p (c i)").bitcast(I32))
+        for q in range(QUADS):
+            nc.sync.dma_start(
+                w3_plane[32 * q : 32 * q + 4, :].bitcast(I32), w3_scales[0, 4 * q : 4 * q + 4, :].bitcast(I32)
+            )
+        for i in range(PAIRS):
+            nc.sync.dma_start(
+                floor[i][:], least[2 * P * i : 2 * P * (i + 1), :].rearrange("(u p) j -> p u j", p=P)
+            )
+
+        v_rows = keep.tile([P, S], U8, name="v_rows", align_bytes=64)
+        nc.vector.tensor_copy(v_rows[:], tab_rows[:].indirect(offsets[:]))
+        for a in range(PASSES):
+            for q in range(QUADS):
+                first = 64 * a + 16 * q
+                nc.gpsimd.dma_start(
+                    v_plane[a][32 * q : 32 * q + 4, :].bitcast(I32), v_rows[first : first + 16 : 4, :].bitcast(I32)
+                )
+
+        w2_codes = keep.tile([P, PASSES, 2 * H], U8, name="w2_codes", align_bytes=64)
+        w2_plane = keep.tile([P, PASSES, H], U8, name="w2_plane", align_bytes=64)
+        nc.vector.tensor_copy(
+            w2_codes[:].bitcast(U16).rearrange("p a (t m) -> p a t m", t=PACK),
+            w2_raw[:].bitcast(U16).rearrange("p a (m t) -> p a t m", t=PACK),
+        )
+        nc.vector.tensor_copy(
+            w2_plane[:].rearrange("p a (t m) -> p a t m", t=PACK),
+            w2_plane_raw[:].rearrange("p a (m t) -> p a t m", t=PACK),
+        )
+
+        w1_codes = [keep.tile([P, H], U32, name=f"w1_codes{a}", align_bytes=64) for a in range(PASSES)]
+        w1_plane = [keep.tile([P, H], U8, name=f"w1_plane{a}", align_bytes=64) for a in range(PASSES)]
+        for a in range(PASSES):
+            w1_bf = work.tile([P, PACK * H], BF16, name="w1_bf", align_bytes=64)
+            nc.scalar.copy(
+                w1_bf[:].rearrange("p (t m j) -> p m t j", t=PACK, j=PACK),
+                w1_raw[a][:].rearrange("p j (m t) -> p m t j", t=PACK),
+            )
+            nc.vector.quantize_mx(w1_codes[a][:].bitcast(E4M3), w1_plane[a][:], w1_bf[:])
+
+        v_codes = {}
+        for a in range(PASSES):
+            for s in range(S // SLICE):
+                v_codes[a, s] = keep.tile([P, SLICE], U32, name=f"v_codes{a}_{s}", align_bytes=64)
+                nc.vector.tensor_copy(
+                    v_codes[a, s][:], tab[a][:].indirect(offsets[:, s * SLICE // 16 : (s + 1) * SLICE // 16])
+                )
+
+        h_tiles = {sp: keep.tile([P, PACK, sp[1] - sp[0]], F32, name=f"h{sp[0]}") for sp in H_STORES}
+        y_tiles = {sp: keep.tile([P, N // P, sp[1] - sp[0]], F32, name=f"y{sp[0]}") for sp in Y_STORES}
+        h_codes = keep.tile([P, S], U32, name="h_codes", align_bytes=64)
+        h_plane = keep.tile([P, S], U8, name="h_plane", align_bytes=64)
+        out_1_rows = out_1.rearrange("(p t) j -> p t j", t=PACK)
+        out_0_rows = out_0.rearrange("(i p) j -> p i j", p=P)
+        out_2_words = out_2[0].rearrange("p m t -> p (m t)").bitcast(I32)
+
+        amp = {}
+        resp = {}
+        h_bf = {}
+        match = {}
+
+        def front(c):
+            c0, c1 = CHUNKS[c]
+            width = c1 - c0
+            s = c0 // SLICE
+            in_slice = slice(c0 - s * SLICE, c1 - s * SLICE)
+            square = [work.tile([P, 2, 256], F32, name=f"square{u}") for u in range(2)]
+            root = [work.tile([P, 2, 256], F32, name=f"root{u}") for u in range(2)]
+            for u in range(2):
+                resp[c, u] = work.tile([P, 2, 256], F32, name=f"resp{u}")
+                pos = psum.tile([P, 2, 256], F32, name=f"pos{u}")
+                for e in range(2):
+                    t = 2 * u + e
+                    for a in range(PASSES):
+                        nc.tensor.matmul_mx(
+                            pos[:, e, 0:width],
+                            lhsT=w1_codes[a][:, P * t : P * (t + 1)].bitcast(E4M3),
+                            lhsT_scale=w1_plane[a][:, P * t : P * (t + 1)],
+                            rhs=v_codes[a, s][:, in_slice].bitcast(E4M3),
+                            rhs_scale=v_plane[a][:, c0:c1],
+                            start=(a == 0),
+                            stop=(a == PASSES - 1),
+                        )
+                for e in range(2):
+                    t = 2 * u + e
+                    nc.scalar.activation(
+                        square[u][:, e, 0:width], pos[:, e, 0:width], ACT.Square, bias=centre[:, t : t + 1], scale=-1.0
+                    )
+            if c0 % SLICE == 0:
+                for t in range(PACK):
+                    amp[s, t] = psum.tile([P, SLICE], F32, name=f"amp{t}")
+                    for a in range(PASSES):
+                        nc.tensor.matmul_mx(
+                            amp[s, t][:],
+                            lhsT=w2_codes[:, a, 2 * P * t : 2 * P * (t + 1)].bitcast(E2M1),
+                            lhsT_scale=w2_plane[:, a, P * t : P * (t + 1)],
+                            rhs=v_codes[a, s][:].bitcast(E4M3),
+                            rhs_scale=v_plane[a][:, s * SLICE : (s + 1) * SLICE],
+                            start=(a == 0),
+                            stop=(a == PASSES - 1),
+                        )
+            for u in range(2):
+                nc.scalar.activation(
+                    root[u][:, :, 0:width], square[u][:, :, 0:width], ACT.Abs_reciprocal_sqrt, bias=one[:]
+                )
+            for u in range(2):
+                if c in DVE_SQUARE:
+                    nc.vector.tensor_tensor(
+                        resp[c, u][:, :, 0:width], root[u][:, :, 0:width], root[u][:, :, 0:width], ALU.mult
+                    )
+                else:
+                    nc.scalar.activation(resp[c, u][:, :, 0:width], root[u][:, :, 0:width], ACT.Square)
+
+        def respond(c):
+            c0, c1 = CHUNKS[c]
+            width = c1 - c0
+            s = c0 // SLICE
+            in_slice = slice(c0 - s * SLICE, c1 - s * SLICE)
+            h_span = holder(H_STORES, c0)
+            h_cols = slice(c0 - h_span[0], c1 - h_span[0])
+            h_tile = h_tiles[h_span]
+            for t in range(PACK):
+                nc.vector.tensor_tensor(
+                    h_tile[:, t, h_cols], amp[s, t][:, in_slice], resp[c, t // 2][:, t % 2, 0:width], ALU.mult
+                )
+            h_bf[c] = work.tile([P, PACK * 256], BF16, name="h_bf", align_bytes=64)
+            if True:
+                (nc.scalar.copy if c in ACT_ROUND else nc.vector.tensor_copy)(
+                    h_bf[c][:, 0 : PACK * width].rearrange("p (c i t) -> p c t i", i=4, t=PACK),
+                    h_tile[:, :, h_cols].rearrange("p t (c i) -> p c t i", i=4),
+                )
+            if c1 == h_span[1]:
+                nc.sync.dma_start(out_1_rows[:, :, h_span[0] : h_span[1]], h_tile[:])
+
+        def quantise(c):
+            c0, c1 = CHUNKS[c]
+            nc.vector.quantize_mx(
+                h_codes[:, c0:c1].bitcast(E4M3), h_plane[:, c0:c1], h_bf[c][:, 0 : PACK * (c1 - c0)]
+            )
+            code_span = holder(CODE_STORES, c0)
+            if c1 == code_span[1]:
+                nc.sync.dma_start(
+                    out_2_words[:, code_span[0] : code_span[1]], h_codes[:, code_span[0] : code_span[1]].bitcast(I32)
+                )
+            if c1 == S:
+                for q in range(QUADS):
+                    nc.scalar.dma_start(
+                        out_3[0, 4 * q : 4 * q + 4, :].bitcast(I32), h_plane[32 * q : 32 * q + 4, :].bitcast(I32)
+                    )
+
+        def score(c, i):
+            c0, c1 = CHUNKS[c]
+            match[c, i] = psum.tile([P, 2, 256], F32, name=f"match{(PAIRS * c + i) % 2}")
+            for e in range(2):
+                n0 = P * (2 * i + e)
+                nc.tensor.matmul_mx(
+                    match[c, i][:, e, 0 : c1 - c0],
+                    lhsT=w3_codes[:, n0 : n0 + P].bitcast(E4M3),
+                    lhsT_scale=w3_plane[:, n0 : n0 + P],
+                    rhs=h_codes[:, c0:c1].bitcast(E4M3),
+                    rhs_scale=h_plane[:, c0:c1],
+                    start=True,
+                    stop=True,
+                )
+
+        def keep_above(c, i):
+            c0, c1 = CHUNKS[c]
+            y_span = holder(Y_STORES, c0)
+            y_tile = y_tiles[y_span]
+            nc.vector.tensor_tensor(
+                y_tile[:, 2 * i : 2 * i + 2, c0 - y_span[0] : c1 - y_span[0]],
+                match[c, i][:, :, 0 : c1 - c0],
+                floor[i][:, :, c0:c1],
+                ALU.max,
+            )
+            if c1 == S:
+                nc.sync.dma_start(
+                    out_0_rows[:, 2 * i : 2 * i + 2, y_span[0] : y_span[1]], y_tile[:, 2 * i : 2 * i + 2, :]
+                )
+            elif i == PAIRS - 1 and c1 == y_span[1]:
+                nc.sync.dma_start(out_0_rows[:, :, y_span[0] : y_span[1]], y_tile[:])
+
+        front(0)
+        respond(0)
+        for c in range(len(CHUNKS)):
+            more = c + 1 < len(CHUNKS)
+            if more:
+                front(c + 1)
+            quantise(c)
+            score(c, 0)
+            score(c, 1)
+            if more:
+                respond(c + 1)
+            keep_above(c, 0)
+            score(c, 2)
+            keep_above(c, 1)
+            keep_above(c, 2)

@@ -22,8 +22,8 @@ PASSES = K // (P * PACK)
 QUADS = 4
 SLICE = 512
 CHUNKS = [(0, 256), (256, 512), (512, 768), (768, 896), (896, 1024)]
-H_STORES = CHUNKS
-Y_STORES = CHUNKS
+H_STORES = [(0, 512), (512, 768), (768, 1024)]
+Y_STORES = [(0, 256), (256, 512), (512, 768), (768, 1024)]
 CODE_STORES = [(0, 512), (512, 1024)]
 ACT_ROUND = (2, 3)
 DVE_SQUARE = (0,)
@@ -123,8 +123,8 @@ def tile_list_lidar_radar_resonance_kernel(
         for a in range(PASSES):
             w1_bf = work.tile([P, PACK * H], BF16, name="w1_bf", align_bytes=64)
             nc.scalar.copy(
-                w1_bf[:].rearrange("p (t m j) -> p m t j", t=PACK, j=PACK),
-                w1_raw[a][:].rearrange("p j (m t) -> p m t j", t=PACK),
+                w1_bf[:].rearrange("p (t m j) -> p t m j", t=PACK, j=PACK),
+                w1_raw[a][:].rearrange("p j (m t) -> p t m j", t=PACK),
             )
             nc.vector.quantize_mx(w1_codes[a][:].bitcast(E4M3), w1_plane[a][:], w1_bf[:])
 
@@ -216,8 +216,8 @@ def tile_list_lidar_radar_resonance_kernel(
             h_bf[c] = work.tile([P, PACK * 256], BF16, name="h_bf", align_bytes=64)
             if True:
                 (nc.scalar.copy if c in ACT_ROUND else nc.vector.tensor_copy)(
-                    h_bf[c][:, 0 : PACK * width].rearrange("p (c i t) -> p c t i", i=4, t=PACK),
-                    h_tile[:, :, h_cols].rearrange("p t (c i) -> p c t i", i=4),
+                    h_bf[c][:, 0 : PACK * width].rearrange("p (c t) -> p c t", t=PACK),
+                    h_tile[:, :, h_cols].rearrange("p t c -> p c t"),
                 )
             if c1 == h_span[1]:
                 nc.sync.dma_start(out_1_rows[:, :, h_span[0] : h_span[1]], h_tile[:])

@@ -79,20 +79,18 @@ def tile_list_lidar_radar_resonance_kernel(
             tab_rows[0:P:4, :].bitcast(I32), tab_scales.rearrange("a q t -> (a q) t").bitcast(I32)
         )
         nc.sync.dma_start(w2_raw[:].bitcast(I32), w2_words.rearrange("a p b -> p a b").bitcast(I32))
-        for q in range(QUADS):
+        for r in range(4):
             nc.sync.dma_start(
-                w2_plane_raw[32 * q : 32 * q + 4, :, :].bitcast(I32),
-                w2_scales[:, 4 * q : 4 * q + 4, :].rearrange("a r c -> r a c").bitcast(I32),
+                w2_plane_raw[r:P:32, :, :].bitcast(I32),
+                w2_scales[:, r:16:4, :].rearrange("a q c -> q a c").bitcast(I32),
             )
         load_w1(1)
         for a in range(PASSES):
             nc.sync.dma_start(tab[a][:].bitcast(I32), tab_words[a].rearrange("p t i -> p (t i)").bitcast(I32))
         nc.sync.dma_start(centre[:], centres.rearrange("(p t) -> p t", t=PACK))
         nc.sync.dma_start(w3_codes[:].bitcast(I32), w3_words[0].rearrange("p c i -> p (c i)").bitcast(I32))
-        for q in range(QUADS):
-            nc.sync.dma_start(
-                w3_plane[32 * q : 32 * q + 4, :].bitcast(I32), w3_scales[0, 4 * q : 4 * q + 4, :].bitcast(I32)
-            )
+        for r in range(4):
+            nc.sync.dma_start(w3_plane[r:P:32, :].bitcast(I32), w3_scales[0, r:16:4, :].bitcast(I32))
         for i in range(PAIRS):
             nc.sync.dma_start(
                 floor[i][:], least[2 * P * i : 2 * P * (i + 1), :].rearrange("(u p) j -> p u j", p=P)
@@ -101,10 +99,9 @@ def tile_list_lidar_radar_resonance_kernel(
         v_rows = keep.tile([P, S], U8, name="v_rows", align_bytes=64)
         nc.vector.tensor_copy(v_rows[:], tab_rows[:].indirect(offsets[:]))
         for a in range(PASSES):
-            for q in range(QUADS):
-                first = 64 * a + 16 * q
-                nc.gpsimd.dma_start(
-                    v_plane[a][32 * q : 32 * q + 4, :].bitcast(I32), v_rows[first : first + 16 : 4, :].bitcast(I32)
+            for r in range(4):
+                (nc.scalar if a == 0 else nc.gpsimd).dma_start(
+                    v_plane[a][r:P:32, :].bitcast(I32), v_rows[64 * a + 4 * r : 64 * (a + 1) : 16, :].bitcast(I32)
                 )
 
         w2_codes = keep.tile([P, PASSES, 2 * H], U8, name="w2_codes", align_bytes=64)
@@ -233,10 +230,8 @@ def tile_list_lidar_radar_resonance_kernel(
                     out_2_words[:, code_span[0] : code_span[1]], h_codes[:, code_span[0] : code_span[1]].bitcast(I32)
                 )
             if c1 == S:
-                for q in range(QUADS):
-                    nc.scalar.dma_start(
-                        out_3[0, 4 * q : 4 * q + 4, :].bitcast(I32), h_plane[32 * q : 32 * q + 4, :].bitcast(I32)
-                    )
+                for r in range(4):
+                    nc.scalar.dma_start(out_3[0, r:16:4, :].bitcast(I32), h_plane[r:P:32, :].bitcast(I32))
 
         def score(c, i):
             c0, c1 = CHUNKS[c]

@@ -19,22 +19,14 @@ ALU = mybir.AluOpType
 P = 128
 PACK = 4
 PASSES = K // (P * PACK)
-QUADS = 4
-SLICE = 512
-CHUNKS = [(0, 256), (256, 512), (512, 768), (768, 896), (896, 1024)]
-H_STORES = [(0, 512), (512, 768), (768, 1024)]
-Y_STORES = [(0, 256), (256, 512), (512, 768), (768, 1024)]
-CODE_STORES = [(0, 512), (512, 1024)]
-ACT_ROUND = (2, 3)
-DVE_SQUARE = (0,)
+HALF = 512
+CHUNKS = [(0, 256), (256, 512), (512, 768), (768, 1024)]
+WIDEST = 256
+VECTOR_SQUARES = (0,)
+SCALAR_ROUNDS = (3,)
+GPSIMD_ROUNDS = ()
 PAIRS = N // (2 * P)
-
-
-def holder(spans, col):
-    for span in spans:
-        if span[0] <= col < span[1]:
-            return span
-    raise ValueError(col)
+ROW_STEP = 4
 
 
 def tile_list_lidar_radar_resonance_kernel(
@@ -51,191 +43,225 @@ def tile_list_lidar_radar_resonance_kernel(
         tab_rows = keep.tile([P, T], U8, name="tab_rows", align_bytes=64)
         w2_plane_raw = keep.tile([P, PASSES, H], U8, name="w2_plane_raw", align_bytes=64)
         w3_plane = keep.tile([P, N], U8, name="w3_plane", align_bytes=64)
-        v_plane = [keep.tile([P, S], U8, name=f"v_plane{a}", align_bytes=64) for a in range(PASSES)]
+        v_plane = keep.tile([P, PASSES * S], U8, name="v_plane", align_bytes=64)
         one = keep.tile([P, 1], F32, name="one")
-        warm = keep.tile([P, 1], F32, name="warm")
+        seed = keep.tile([P, 1], F32, name="seed", align_bytes=64)
+        centre = keep.tile([P, PACK], F32, name="centre")
 
         nc.vector.memset(tab_rows[:].bitcast(I32), 0)
         nc.vector.memset(w2_plane_raw[:].rearrange("p a c -> p (a c)").bitcast(I32), 0)
-        nc.vector.memset(one[:], 1.0)
-        nc.vector.memset(w3_plane[:].bitcast(I32), 0)
-        for a in range(PASSES):
-            nc.vector.memset(v_plane[a][:].bitcast(I32), 0)
-        nc.scalar.activation(warm[:], one[:], ACT.Abs_reciprocal_sqrt)
+        nc.vector.memset(seed[:], 1.0)
+        nc.vector.memset(v_plane[:].bitcast(I32), 0)
+        nc.gpsimd.memset(w3_plane[:].bitcast(I32), 0)
+        nc.scalar.activation(one[:], seed[:], ACT.Abs_reciprocal_sqrt)
 
-        w1_raw = [keep.tile([P, PACK, H], F32, name=f"w1_raw{a}") for a in range(PASSES)]
-        tab = [keep.tile([P, T], U32, name=f"tab{a}", align_bytes=64) for a in range(PASSES)]
         w2_raw = keep.tile([P, PASSES, 2 * H], U8, name="w2_raw", align_bytes=64)
-        w3_codes = keep.tile([P, N], U32, name="w3_codes", align_bytes=64)
-        centre = keep.tile([P, PACK], F32, name="centre")
-        floor = [keep.tile([P, 2, S], F32, name=f"floor{i}") for i in range(PAIRS)]
+        w1_codes = [keep.tile([P, H], U32, name=f"w1_codes{a}", align_bytes=64) for a in range(PASSES)]
+        w1_plane = [keep.tile([P, H], U8, name=f"w1_plane{a}", align_bytes=64) for a in range(PASSES)]
+        tab = {}
+        w1_raw = {}
 
-        def load_w1(a):
+        def load_w1(a, tag):
+            w1_raw[a] = keep.tile([P, PACK, H], F32, name=f"w1_raw{a}", tag=tag, align_bytes=64)
             nc.sync.dma_start(w1_raw[a][:], w1[512 * a : 512 * (a + 1), :].rearrange("(p j) c -> p j c", j=PACK))
 
+        def load_tab(a, tag):
+            tab[a] = keep.tile([P, T], U32, name=f"tab{a}", tag=tag, align_bytes=64)
+            nc.sync.dma_start(tab[a][:].bitcast(I32), tab_words[a].rearrange("p t i -> p (t i)").bitcast(I32))
+
+        def quantise_w1(a):
+            w1_bf = keep.tile([P, PACK * H], BF16, name=f"w1_bf{a}", align_bytes=64)
+            nc.scalar.copy(
+                w1_bf[:].rearrange("p (t m j) -> p m j t", t=PACK, j=PACK),
+                w1_raw[a][:].rearrange("p j (m t) -> p m j t", t=PACK),
+            )
+            nc.vector.quantize_mx(w1_codes[a][:].bitcast(E4M3), w1_plane[a][:], w1_bf[:])
+
         nc.sync.dma_start(offsets[:], offs)
-        load_w1(0)
-        nc.sync.dma_start(
-            tab_rows[0:P:4, :].bitcast(I32), tab_scales.rearrange("a q t -> (a q) t").bitcast(I32)
-        )
+        load_w1(0, "w1_raw0")
         nc.sync.dma_start(w2_raw[:].bitcast(I32), w2_words.rearrange("a p b -> p a b").bitcast(I32))
+        nc.sync.dma_start(
+            tab_rows[0:P:ROW_STEP, :].bitcast(I32),
+            tab_scales.bitcast(I32).rearrange("a q t -> q a t"),
+        )
         for r in range(4):
             nc.sync.dma_start(
                 w2_plane_raw[r:P:32, :, :].bitcast(I32),
                 w2_scales[:, r:16:4, :].rearrange("a q c -> q a c").bitcast(I32),
             )
-        load_w1(1)
-        for a in range(PASSES):
-            nc.sync.dma_start(tab[a][:].bitcast(I32), tab_words[a].rearrange("p t i -> p (t i)").bitcast(I32))
-        nc.sync.dma_start(centre[:], centres.rearrange("(p t) -> p t", t=PACK))
-        nc.sync.dma_start(w3_codes[:].bitcast(I32), w3_words[0].rearrange("p c i -> p (c i)").bitcast(I32))
+        load_tab(0, "seed")
+        nc.gpsimd.dma_start(centre[:], centres.rearrange("(p t) -> p t", t=PACK))
         for r in range(4):
-            nc.sync.dma_start(w3_plane[r:P:32, :].bitcast(I32), w3_scales[0, r:16:4, :].bitcast(I32))
-        for i in range(PAIRS):
-            nc.sync.dma_start(
-                floor[i][:], least[2 * P * i : 2 * P * (i + 1), :].rearrange("(u p) j -> p u j", p=P)
-            )
-
-        v_rows = keep.tile([P, S], U8, name="v_rows", align_bytes=64)
-        nc.vector.tensor_copy(v_rows[:], tab_rows[:].indirect(offsets[:]))
-        for a in range(PASSES):
-            for r in range(4):
-                (nc.scalar if a == 0 else nc.gpsimd).dma_start(
-                    v_plane[a][r:P:32, :].bitcast(I32), v_rows[64 * a + 4 * r : 64 * (a + 1) : 16, :].bitcast(I32)
-                )
+            nc.gpsimd.dma_start(w3_plane[r:P:32, :].bitcast(I32), w3_scales[0, r:16:4, :].bitcast(I32))
 
         w2_codes = keep.tile([P, PASSES, 2 * H], U8, name="w2_codes", align_bytes=64)
         w2_plane = keep.tile([P, PASSES, H], U8, name="w2_plane", align_bytes=64)
         nc.vector.tensor_copy(
-            w2_codes[:].bitcast(U16).rearrange("p a (t m) -> p a t m", t=PACK),
-            w2_raw[:].bitcast(U16).rearrange("p a (m t) -> p a t m", t=PACK),
+            w2_codes[:].bitcast(U16).rearrange("p a (t m) -> p a m t", t=PACK),
+            w2_raw[:].bitcast(U16).rearrange("p a (m t) -> p a m t", t=PACK),
         )
-        nc.vector.tensor_copy(
-            w2_plane[:].rearrange("p a (t m) -> p a t m", t=PACK),
-            w2_plane_raw[:].rearrange("p a (m t) -> p a t m", t=PACK),
-        )
+        load_w1(1, "w2_raw")
 
-        w1_codes = [keep.tile([P, H], U32, name=f"w1_codes{a}", align_bytes=64) for a in range(PASSES)]
-        w1_plane = [keep.tile([P, H], U8, name=f"w1_plane{a}", align_bytes=64) for a in range(PASSES)]
-        for a in range(PASSES):
-            w1_bf = work.tile([P, PACK * H], BF16, name="w1_bf", align_bytes=64)
-            nc.scalar.copy(
-                w1_bf[:].rearrange("p (t m j) -> p t m j", t=PACK, j=PACK),
-                w1_raw[a][:].rearrange("p j (m t) -> p t m j", t=PACK),
+
+        v_rows = keep.tile([P, S], U8, name="v_rows", align_bytes=64)
+        nc.vector.tensor_copy(v_rows[:], tab_rows[:].indirect(offsets[:]))
+        quantise_w1(0)
+        for q in range(4):
+            nc.sync.dma_start(
+                v_plane[32 * q : 32 * q + 4, :].bitcast(I32), v_rows[32 * q : 32 * (q + 1) : ROW_STEP, :].bitcast(I32)
             )
-            nc.vector.quantize_mx(w1_codes[a][:].bitcast(E4M3), w1_plane[a][:], w1_bf[:])
+
+        load_tab(1, "w1_bf0")
+        nc.vector.tensor_copy(
+            w2_plane[:].rearrange("p a (t m) -> p a m t", t=PACK),
+            w2_plane_raw[:].rearrange("p a (m t) -> p a m t", t=PACK),
+        )
+        quantise_w1(1)
+        w3_codes = keep.tile([P, N], U32, name="w3_codes", tag="v_rows", align_bytes=64)
+        nc.sync.dma_start(w3_codes[:].bitcast(I32), w3_words[0].rearrange("p c i -> p (c i)").bitcast(I32))
+
+        floors = keep.tile([P, PAIRS * 2 * S], F32, name="floors", tag="w2_raw", align_bytes=64)
+        floor = [floors[:, 2 * S * i : 2 * S * (i + 1)].rearrange("p (u j) -> p u j", u=2) for i in range(PAIRS)]
+        for i in range(PAIRS):
+            nc.sync.dma_start(floor[i], least[2 * P * i : 2 * P * (i + 1), :].rearrange("(u p) j -> p u j", p=P))
 
         v_codes = {}
         for a in range(PASSES):
-            for s in range(S // SLICE):
-                v_codes[a, s] = keep.tile([P, SLICE], U32, name=f"v_codes{a}_{s}", align_bytes=64)
+            for s in range(S // HALF):
+                v_codes[a, s] = keep.tile([P, HALF], U32, name=f"v_codes{a}_{s}", align_bytes=64)
                 nc.vector.tensor_copy(
-                    v_codes[a, s][:], tab[a][:].indirect(offsets[:, s * SLICE // 16 : (s + 1) * SLICE // 16])
+                    v_codes[a, s][:], tab[a][:].indirect(offsets[:, s * HALF // 16 : (s + 1) * HALF // 16])
                 )
 
-        h_tiles = {sp: keep.tile([P, PACK, sp[1] - sp[0]], F32, name=f"h{sp[0]}") for sp in H_STORES}
-        y_tiles = {sp: keep.tile([P, N // P, sp[1] - sp[0]], F32, name=f"y{sp[0]}") for sp in Y_STORES}
+        h_tiles = [keep.tile([P, PACK, HALF], F32, name=f"h{s}") for s in range(S // HALF)]
+        y_tiles = {(s, i): keep.tile([P, 2, HALF], F32, name=f"y{s}_{i}") for s in range(S // HALF) for i in range(PAIRS)}
         h_codes = keep.tile([P, S], U32, name="h_codes", align_bytes=64)
         h_plane = keep.tile([P, S], U8, name="h_plane", align_bytes=64)
         out_1_rows = out_1.rearrange("(p t) j -> p t j", t=PACK)
         out_0_rows = out_0.rearrange("(i p) j -> p i j", p=P)
         out_2_words = out_2[0].rearrange("p m t -> p (m t)").bitcast(I32)
 
+        pos = {}
         amp = {}
+        root = {}
         resp = {}
         h_bf = {}
         match = {}
 
-        def front(c):
-            c0, c1 = CHUNKS[c]
-            width = c1 - c0
-            s = c0 // SLICE
-            in_slice = slice(c0 - s * SLICE, c1 - s * SLICE)
-            square = [work.tile([P, 2, 256], F32, name=f"square{u}") for u in range(2)]
-            root = [work.tile([P, 2, 256], F32, name=f"root{u}") for u in range(2)]
-            for u in range(2):
-                resp[c, u] = work.tile([P, 2, 256], F32, name=f"resp{u}")
-                pos = psum.tile([P, 2, 256], F32, name=f"pos{u}")
-                for e in range(2):
-                    t = 2 * u + e
-                    for a in range(PASSES):
-                        nc.tensor.matmul_mx(
-                            pos[:, e, 0:width],
-                            lhsT=w1_codes[a][:, P * t : P * (t + 1)].bitcast(E4M3),
-                            lhsT_scale=w1_plane[a][:, P * t : P * (t + 1)],
-                            rhs=v_codes[a, s][:, in_slice].bitcast(E4M3),
-                            rhs_scale=v_plane[a][:, c0:c1],
-                            start=(a == 0),
-                            stop=(a == PASSES - 1),
-                        )
-                for e in range(2):
-                    t = 2 * u + e
-                    nc.scalar.activation(
-                        square[u][:, e, 0:width], pos[:, e, 0:width], ACT.Square, bias=centre[:, t : t + 1], scale=-1.0
-                    )
-            if c0 % SLICE == 0:
+        def pos_pass(out, a, t, c0, c1):
+            s = c0 // HALF
+            nc.tensor.matmul_mx(
+                out,
+                lhsT=w1_codes[a][:, P * t : P * (t + 1)].bitcast(E4M3),
+                lhsT_scale=w1_plane[a][:, P * t : P * (t + 1)],
+                rhs=v_codes[a, s][:, c0 - s * HALF : c1 - s * HALF].bitcast(E4M3),
+                rhs_scale=v_plane[:, a * S + c0 : a * S + c1],
+                start=(a == 0),
+                stop=(a == PASSES - 1),
+            )
+
+        def amp_pass(a, t, s):
+            nc.tensor.matmul_mx(
+                amp[s, t][:],
+                lhsT=w2_codes[:, a, 2 * P * t : 2 * P * (t + 1)].bitcast(E2M1),
+                lhsT_scale=w2_plane[:, a, P * t : P * (t + 1)],
+                rhs=v_codes[a, s][:].bitcast(E4M3),
+                rhs_scale=v_plane[:, a * S + s * HALF : a * S + (s + 1) * HALF],
+                start=(a == 0),
+                stop=(a == PASSES - 1),
+            )
+
+        def first_half_products():
+            banks = [psum.tile([P, HALF], F32, name=f"front{t}") for t in range(PACK)]
+            for t in range(PACK):
+                amp[0, t] = psum.tile([P, HALF], F32, name=f"amp{t}")
+                for c, (c0, c1) in enumerate(CHUNKS):
+                    if c1 <= HALF:
+                        pos[c, t] = banks[t][:, c0:c1]
+            for a in range(PASSES):
                 for t in range(PACK):
-                    amp[s, t] = psum.tile([P, SLICE], F32, name=f"amp{t}")
-                    for a in range(PASSES):
-                        nc.tensor.matmul_mx(
-                            amp[s, t][:],
-                            lhsT=w2_codes[:, a, 2 * P * t : 2 * P * (t + 1)].bitcast(E2M1),
-                            lhsT_scale=w2_plane[:, a, P * t : P * (t + 1)],
-                            rhs=v_codes[a, s][:].bitcast(E4M3),
-                            rhs_scale=v_plane[a][:, s * SLICE : (s + 1) * SLICE],
-                            start=(a == 0),
-                            stop=(a == PASSES - 1),
-                        )
+                    pos_pass(banks[t][:], a, t, 0, HALF)
+                for t in range(PACK):
+                    amp_pass(a, t, 0)
+
+        def second_half_amp():
+            for t in range(PACK):
+                amp[1, t] = psum.tile([P, HALF], F32, name=f"amp{t}")
+                for a in range(PASSES):
+                    amp_pass(a, t, 1)
+
+        def chunk_pos(c):
+            c0, c1 = CHUNKS[c]
             for u in range(2):
+                bank = psum.tile([P, 2, WIDEST], F32, name=f"front{u}")
+                for e in range(2):
+                    pos[c, 2 * u + e] = bank[:, e, 0 : c1 - c0]
+                    for a in range(PASSES):
+                        pos_pass(pos[c, 2 * u + e], a, 2 * u + e, c0, c1)
+
+        def roots(c):
+            width = CHUNKS[c][1] - CHUNKS[c][0]
+            square = [work.tile([P, 2, width], F32, name=f"square{u}") for u in range(2)]
+            for t in range(PACK):
                 nc.scalar.activation(
-                    root[u][:, :, 0:width], square[u][:, :, 0:width], ACT.Abs_reciprocal_sqrt, bias=one[:]
+                    square[t // 2][:, t % 2, :], pos[c, t], ACT.Square, bias=centre[:, t : t + 1], scale=-1.0
                 )
             for u in range(2):
-                if c in DVE_SQUARE:
-                    nc.vector.tensor_tensor(
-                        resp[c, u][:, :, 0:width], root[u][:, :, 0:width], root[u][:, :, 0:width], ALU.mult
-                    )
-                else:
-                    nc.scalar.activation(resp[c, u][:, :, 0:width], root[u][:, :, 0:width], ACT.Square)
+                root[c, u] = work.tile([P, 2, width], F32, name=f"root{u}")
+                nc.scalar.activation(root[c, u][:], square[u][:], ACT.Abs_reciprocal_sqrt, bias=one[:])
 
-        def respond(c):
+        def responses(c):
+            width = CHUNKS[c][1] - CHUNKS[c][0]
+            for u in range(2):
+                resp[c, u] = work.tile([P, 2, width], F32, name=f"resp{u}")
+                if c in VECTOR_SQUARES:
+                    nc.vector.tensor_tensor(resp[c, u][:], root[c, u][:], root[c, u][:], ALU.mult)
+                else:
+                    nc.scalar.activation(resp[c, u][:], root[c, u][:], ACT.Square)
+
+        def half_cols(c):
             c0, c1 = CHUNKS[c]
-            width = c1 - c0
-            s = c0 // SLICE
-            in_slice = slice(c0 - s * SLICE, c1 - s * SLICE)
-            h_span = holder(H_STORES, c0)
-            h_cols = slice(c0 - h_span[0], c1 - h_span[0])
-            h_tile = h_tiles[h_span]
+            return slice(c0 % HALF, c0 % HALF + c1 - c0)
+
+        def amplify(c):
+            c0, c1 = CHUNKS[c]
+            s = c0 // HALF
             for t in range(PACK):
                 nc.vector.tensor_tensor(
-                    h_tile[:, t, h_cols], amp[s, t][:, in_slice], resp[c, t // 2][:, t % 2, 0:width], ALU.mult
+                    h_tiles[s][:, t, half_cols(c)], amp[s, t][:, half_cols(c)], resp[c, t // 2][:, t % 2, :], ALU.mult
                 )
-            h_bf[c] = work.tile([P, PACK * 256], BF16, name="h_bf", align_bytes=64)
-            if True:
-                (nc.scalar.copy if c in ACT_ROUND else nc.vector.tensor_copy)(
-                    h_bf[c][:, 0 : PACK * width].rearrange("p (c t) -> p c t", t=PACK),
-                    h_tile[:, :, h_cols].rearrange("p t c -> p c t"),
+            if s == 0:
+                nc.sync.dma_start(out_1_rows[:, :, c0:c1], h_tiles[s][:, :, c0:c1])
+            elif c1 == S:
+                nc.sync.dma_start(out_1_rows[:, :, HALF:S], h_tiles[s][:])
+
+        def round_h(c):
+            c0, c1 = CHUNKS[c]
+            h_bf[c] = work.tile([P, PACK * (c1 - c0)], BF16, name="h_bf", align_bytes=64)
+            source = h_tiles[c0 // HALF][:, :, half_cols(c)]
+            if c in GPSIMD_ROUNDS:
+                nc.gpsimd.tensor_scalar(
+                    h_bf[c][:].rearrange("p (c t) -> p c t", t=PACK), source.rearrange("p t c -> p c t"),
+                    1.0, 0.0, ALU.mult, ALU.add,
                 )
-            if c1 == h_span[1]:
-                nc.sync.dma_start(out_1_rows[:, :, h_span[0] : h_span[1]], h_tile[:])
+            else:
+                (nc.scalar.copy if c in SCALAR_ROUNDS else nc.vector.tensor_copy)(
+                    h_bf[c][:].rearrange("p (c i t) -> p c t i", t=PACK, i=4),
+                    source.rearrange("p t (c i) -> p c t i", i=4),
+                )
 
         def quantise(c):
             c0, c1 = CHUNKS[c]
-            nc.vector.quantize_mx(
-                h_codes[:, c0:c1].bitcast(E4M3), h_plane[:, c0:c1], h_bf[c][:, 0 : PACK * (c1 - c0)]
-            )
-            code_span = holder(CODE_STORES, c0)
-            if c1 == code_span[1]:
-                nc.sync.dma_start(
-                    out_2_words[:, code_span[0] : code_span[1]], h_codes[:, code_span[0] : code_span[1]].bitcast(I32)
-                )
+            nc.vector.quantize_mx(h_codes[:, c0:c1].bitcast(E4M3), h_plane[:, c0:c1], h_bf[c][:])
+            if c1 % HALF == 0:
+                nc.sync.dma_start(out_2_words[:, c1 - HALF : c1], h_codes[:, c1 - HALF : c1].bitcast(I32))
             if c1 == S:
                 for r in range(4):
                     nc.scalar.dma_start(out_3[0, r:16:4, :].bitcast(I32), h_plane[r:P:32, :].bitcast(I32))
 
         def score(c, i):
             c0, c1 = CHUNKS[c]
-            match[c, i] = psum.tile([P, 2, 256], F32, name=f"match{(PAIRS * c + i) % 2}")
+            match[c, i] = psum.tile([P, 2, WIDEST], F32, name=f"front{(2 + (PAIRS * c + i) % 2) if c < 2 else (PAIRS * c + i) % 4}")
             for e in range(2):
                 n0 = P * (2 * i + e)
                 nc.tensor.matmul_mx(
@@ -250,33 +276,40 @@ def tile_list_lidar_radar_resonance_kernel(
 
         def keep_above(c, i):
             c0, c1 = CHUNKS[c]
-            y_span = holder(Y_STORES, c0)
-            y_tile = y_tiles[y_span]
+            s = c0 // HALF
             nc.vector.tensor_tensor(
-                y_tile[:, 2 * i : 2 * i + 2, c0 - y_span[0] : c1 - y_span[0]],
-                match[c, i][:, :, 0 : c1 - c0],
-                floor[i][:, :, c0:c1],
-                ALU.max,
+                y_tiles[s, i][:, :, half_cols(c)], match[c, i][:, :, 0 : c1 - c0], floor[i][:, :, c0:c1], ALU.max
             )
-            if c1 == S:
-                nc.sync.dma_start(
-                    out_0_rows[:, 2 * i : 2 * i + 2, y_span[0] : y_span[1]], y_tile[:, 2 * i : 2 * i + 2, :]
-                )
-            elif i == PAIRS - 1 and c1 == y_span[1]:
-                nc.sync.dma_start(out_0_rows[:, :, y_span[0] : y_span[1]], y_tile[:])
+            if c1 % HALF == 0:
+                nc.sync.dma_start(out_0_rows[:, 2 * i : 2 * i + 2, s * HALF : (s + 1) * HALF], y_tiles[s, i][:])
 
-        front(0)
-        respond(0)
+        first_half_products()
+        roots(0)
+        responses(0)
+        roots(1)
+        responses(1)
+        amplify(0)
+        round_h(0)
+        quantise(0)
+        chunk_pos(2)
         for c in range(len(CHUNKS)):
             more = c + 1 < len(CHUNKS)
-            if more:
-                front(c + 1)
-            quantise(c)
             score(c, 0)
             score(c, 1)
+            if c + 2 < len(CHUNKS):
+                roots(c + 2)
+                responses(c + 2)
+            if c + 3 < len(CHUNKS):
+                chunk_pos(c + 3)
             if more:
-                respond(c + 1)
+                amplify(c + 1)
+            if c == 0:
+                second_half_amp()
             keep_above(c, 0)
             score(c, 2)
+            if more:
+                round_h(c + 1)
             keep_above(c, 1)
+            if more:
+                quantise(c + 1)
             keep_above(c, 2)

@@ -22,8 +22,10 @@ PASSES = K // (P * PACK)
 HALF = 512
 CHUNKS = [(0, 256), (256, 512), (512, 768), (768, 1024)]
 WIDEST = 256
+H_STORES = [(0, 256), (256, 512), (512, 768), (768, 1024)]
+Y_STORES = [(0, 256), (256, 512), (512, 768), (768, 1024)]
 VECTOR_SQUARES = (0,)
-SCALAR_ROUNDS = (3,)
+SCALAR_ROUNDS = (2, 3)
 GPSIMD_ROUNDS = ()
 PAIRS = N // (2 * P)
 ROW_STEP = 4
@@ -37,6 +39,7 @@ def tile_list_lidar_radar_resonance_kernel(
     with ExitStack() as ctx:
         keep = ctx.enter_context(tc.tile_pool(name="keep", bufs=1))
         work = ctx.enter_context(tc.tile_pool(name="work", bufs=2))
+        relay = ctx.enter_context(tc.tile_pool(name="relay", bufs=1))
         psum = ctx.enter_context(tc.psum_pool(name="psum", bufs=1))
 
         offsets = keep.tile([P, S // 16], U16, name="offsets")
@@ -45,41 +48,44 @@ def tile_list_lidar_radar_resonance_kernel(
         w3_plane = keep.tile([P, N], U8, name="w3_plane", align_bytes=64)
         v_plane = keep.tile([P, PASSES * S], U8, name="v_plane", align_bytes=64)
         one = keep.tile([P, 1], F32, name="one")
-        seed = keep.tile([P, 1], F32, name="seed", align_bytes=64)
+        warm = keep.tile([P, 1], F32, name="warm")
         centre = keep.tile([P, PACK], F32, name="centre")
 
         nc.vector.memset(tab_rows[:].bitcast(I32), 0)
         nc.vector.memset(w2_plane_raw[:].rearrange("p a c -> p (a c)").bitcast(I32), 0)
-        nc.vector.memset(seed[:], 1.0)
+        nc.vector.memset(one[:], 1.0)
         nc.vector.memset(v_plane[:].bitcast(I32), 0)
         nc.gpsimd.memset(w3_plane[:].bitcast(I32), 0)
-        nc.scalar.activation(one[:], seed[:], ACT.Abs_reciprocal_sqrt)
+        nc.scalar.activation(warm[:], one[:], ACT.Abs_reciprocal_sqrt)
 
-        w2_raw = keep.tile([P, PASSES, 2 * H], U8, name="w2_raw", align_bytes=64)
         w1_codes = [keep.tile([P, H], U32, name=f"w1_codes{a}", align_bytes=64) for a in range(PASSES)]
         w1_plane = [keep.tile([P, H], U8, name=f"w1_plane{a}", align_bytes=64) for a in range(PASSES)]
+        w1_raw = [keep.tile([P, PACK, H], F32, name=f"w1_raw{a}") for a in range(PASSES)]
         tab = {}
-        w1_raw = {}
+        v_codes = {}
 
-        def load_w1(a, tag):
-            w1_raw[a] = keep.tile([P, PACK, H], F32, name=f"w1_raw{a}", tag=tag, align_bytes=64)
+        def load_w1(a):
             nc.sync.dma_start(w1_raw[a][:], w1[512 * a : 512 * (a + 1), :].rearrange("(p j) c -> p j c", j=PACK))
 
-        def load_tab(a, tag):
-            tab[a] = keep.tile([P, T], U32, name=f"tab{a}", tag=tag, align_bytes=64)
+        def load_tab(a):
             nc.sync.dma_start(tab[a][:].bitcast(I32), tab_words[a].rearrange("p t i -> p (t i)").bitcast(I32))
 
         def quantise_w1(a):
             w1_bf = keep.tile([P, PACK * H], BF16, name=f"w1_bf{a}", align_bytes=64)
             nc.scalar.copy(
-                w1_bf[:].rearrange("p (t m j) -> p m j t", t=PACK, j=PACK),
-                w1_raw[a][:].rearrange("p j (m t) -> p m j t", t=PACK),
+                w1_bf[:].rearrange("p (t m j) -> p m t j", t=PACK, j=PACK),
+                w1_raw[a][:].rearrange("p j (m t) -> p m t j", t=PACK),
             )
             nc.vector.quantize_mx(w1_codes[a][:].bitcast(E4M3), w1_plane[a][:], w1_bf[:])
 
+        def gather_words(a, s):
+            v_codes[a, s] = keep.tile([P, HALF], U32, name=f"v_codes{a}_{s}", align_bytes=64)
+            nc.vector.tensor_copy(
+                v_codes[a, s][:], tab[a][:].indirect(offsets[:, s * HALF // 16 : (s + 1) * HALF // 16])
+            )
+
         nc.sync.dma_start(offsets[:], offs)
-        load_w1(0, "w1_raw0")
-        nc.sync.dma_start(w2_raw[:].bitcast(I32), w2_words.rearrange("a p b -> p a b").bitcast(I32))
+        load_w1(0)
         nc.sync.dma_start(
             tab_rows[0:P:ROW_STEP, :].bitcast(I32),
             tab_scales.bitcast(I32).rearrange("a q t -> q a t"),
@@ -89,49 +95,48 @@ def tile_list_lidar_radar_resonance_kernel(
                 w2_plane_raw[r:P:32, :, :].bitcast(I32),
                 w2_scales[:, r:16:4, :].rearrange("a q c -> q a c").bitcast(I32),
             )
-        load_tab(0, "seed")
+        load_w1(1)
+        tab[0] = relay.tile([P, T], U32, name="tab0", offset=0, align_bytes=64)
+        load_tab(0)
         nc.gpsimd.dma_start(centre[:], centres.rearrange("(p t) -> p t", t=PACK))
         for r in range(4):
             nc.gpsimd.dma_start(w3_plane[r:P:32, :].bitcast(I32), w3_scales[0, r:16:4, :].bitcast(I32))
 
-        w2_codes = keep.tile([P, PASSES, 2 * H], U8, name="w2_codes", align_bytes=64)
-        w2_plane = keep.tile([P, PASSES, H], U8, name="w2_plane", align_bytes=64)
-        nc.vector.tensor_copy(
-            w2_codes[:].bitcast(U16).rearrange("p a (t m) -> p a m t", t=PACK),
-            w2_raw[:].bitcast(U16).rearrange("p a (m t) -> p a m t", t=PACK),
-        )
-        load_w1(1, "w2_raw")
-
-
         v_rows = keep.tile([P, S], U8, name="v_rows", align_bytes=64)
         nc.vector.tensor_copy(v_rows[:], tab_rows[:].indirect(offsets[:]))
-        quantise_w1(0)
         for q in range(4):
             nc.sync.dma_start(
                 v_plane[32 * q : 32 * q + 4, :].bitcast(I32), v_rows[32 * q : 32 * (q + 1) : ROW_STEP, :].bitcast(I32)
             )
+        tab[1] = keep.tile([P, T], U32, name="tab1", tag="tab_rows", align_bytes=64)
+        load_tab(1)
+        w2_raw = keep.tile([P, PASSES, 2 * H], U8, name="w2_raw", tag="v_rows", align_bytes=64)
+        nc.sync.dma_start(w2_raw[:].bitcast(I32), w2_words.rearrange("a p b -> p a b").bitcast(I32))
 
-        load_tab(1, "w1_bf0")
+        w2_codes = keep.tile([P, PASSES, 2 * H], U8, name="w2_codes", align_bytes=64)
+        w2_plane = keep.tile([P, PASSES, H], U8, name="w2_plane", align_bytes=64)
+        quantise_w1(0)
         nc.vector.tensor_copy(
-            w2_plane[:].rearrange("p a (t m) -> p a m t", t=PACK),
-            w2_plane_raw[:].rearrange("p a (m t) -> p a m t", t=PACK),
+            w2_plane[:].rearrange("p a (t m) -> p a t m", t=PACK),
+            w2_plane_raw[:].rearrange("p a (m t) -> p a t m", t=PACK),
         )
         quantise_w1(1)
-        w3_codes = keep.tile([P, N], U32, name="w3_codes", tag="v_rows", align_bytes=64)
-        nc.sync.dma_start(w3_codes[:].bitcast(I32), w3_words[0].rearrange("p c i -> p (c i)").bitcast(I32))
+        gather_words(0, 1)
+        gather_words(0, 0)
 
-        floors = keep.tile([P, PAIRS * 2 * S], F32, name="floors", tag="w2_raw", align_bytes=64)
+        w3_codes = relay.tile([P, N], U32, name="w3_codes", offset=0, align_bytes=64)
+        nc.sync.dma_start(w3_codes[:].bitcast(I32), w3_words[0].rearrange("p c i -> p (c i)").bitcast(I32))
+        floors = relay.tile([P, PAIRS * 2 * S], F32, name="floors", offset=4 * N, align_bytes=64)
         floor = [floors[:, 2 * S * i : 2 * S * (i + 1)].rearrange("p (u j) -> p u j", u=2) for i in range(PAIRS)]
         for i in range(PAIRS):
             nc.sync.dma_start(floor[i], least[2 * P * i : 2 * P * (i + 1), :].rearrange("(u p) j -> p u j", p=P))
 
-        v_codes = {}
-        for a in range(PASSES):
-            for s in range(S // HALF):
-                v_codes[a, s] = keep.tile([P, HALF], U32, name=f"v_codes{a}_{s}", align_bytes=64)
-                nc.vector.tensor_copy(
-                    v_codes[a, s][:], tab[a][:].indirect(offsets[:, s * HALF // 16 : (s + 1) * HALF // 16])
-                )
+        gather_words(1, 0)
+        nc.vector.tensor_copy(
+            w2_codes[:].bitcast(U16).rearrange("p a (t m) -> p a t m", t=PACK),
+            w2_raw[:].bitcast(U16).rearrange("p a (m t) -> p a t m", t=PACK),
+        )
+        gather_words(1, 1)
 
         h_tiles = [keep.tile([P, PACK, HALF], F32, name=f"h{s}") for s in range(S // HALF)]
         y_tiles = {(s, i): keep.tile([P, 2, HALF], F32, name=f"y{s}_{i}") for s in range(S // HALF) for i in range(PAIRS)}
@@ -181,7 +186,8 @@ def tile_list_lidar_radar_resonance_kernel(
             for a in range(PASSES):
                 for t in range(PACK):
                     pos_pass(banks[t][:], a, t, 0, HALF)
-                for t in range(PACK):
+            for t in range(PACK):
+                for a in range(PASSES):
                     amp_pass(a, t, 0)
 
         def second_half_amp():
@@ -230,10 +236,9 @@ def tile_list_lidar_radar_resonance_kernel(
                 nc.vector.tensor_tensor(
                     h_tiles[s][:, t, half_cols(c)], amp[s, t][:, half_cols(c)], resp[c, t // 2][:, t % 2, :], ALU.mult
                 )
-            if s == 0:
-                nc.sync.dma_start(out_1_rows[:, :, c0:c1], h_tiles[s][:, :, c0:c1])
-            elif c1 == S:
-                nc.sync.dma_start(out_1_rows[:, :, HALF:S], h_tiles[s][:])
+            for j0, j1 in H_STORES:
+                if j1 == c1:
+                    nc.sync.dma_start(out_1_rows[:, :, j0:j1], h_tiles[s][:, :, j0 - s * HALF : j1 - s * HALF])
 
         def round_h(c):
             c0, c1 = CHUNKS[c]
@@ -280,8 +285,11 @@ def tile_list_lidar_radar_resonance_kernel(
             nc.vector.tensor_tensor(
                 y_tiles[s, i][:, :, half_cols(c)], match[c, i][:, :, 0 : c1 - c0], floor[i][:, :, c0:c1], ALU.max
             )
-            if c1 % HALF == 0:
-                nc.sync.dma_start(out_0_rows[:, 2 * i : 2 * i + 2, s * HALF : (s + 1) * HALF], y_tiles[s, i][:])
+            for j0, j1 in Y_STORES:
+                if j1 == c1:
+                    nc.sync.dma_start(
+                        out_0_rows[:, 2 * i : 2 * i + 2, j0:j1], y_tiles[s, i][:, :, j0 - s * HALF : j1 - s * HALF]
+                    )
 
         first_half_products()
         roots(0)

@@ -29,6 +29,7 @@ SCALAR_ROUNDS = (2, 3)
 GPSIMD_ROUNDS = ()
 PAIRS = N // (2 * P)
 ROW_STEP = 4
+ROW = S + H + N // PASSES
 
 
 def tile_list_lidar_radar_resonance_kernel(
@@ -44,18 +45,17 @@ def tile_list_lidar_radar_resonance_kernel(
 
         offsets = keep.tile([P, S // 16], U16, name="offsets")
         tab_rows = keep.tile([P, T], U8, name="tab_rows", align_bytes=64)
-        w2_plane_raw = keep.tile([P, PASSES, H], U8, name="w2_plane_raw", align_bytes=64)
-        w3_plane = keep.tile([P, N], U8, name="w3_plane", align_bytes=64)
-        v_plane = keep.tile([P, PASSES * S], U8, name="v_plane", align_bytes=64)
+        w2_rows = keep.tile([P, H], U8, name="w2_rows", align_bytes=64)
+        rows = keep.tile([P, ROW], U8, name="rows", align_bytes=64)
+        planes = keep.tile([P, PASSES * ROW], U8, name="planes", align_bytes=64)
         one = keep.tile([P, 1], F32, name="one")
         warm = keep.tile([P, 1], F32, name="warm")
         centre = keep.tile([P, PACK], F32, name="centre")
 
         nc.vector.memset(tab_rows[:].bitcast(I32), 0)
-        nc.vector.memset(w2_plane_raw[:].rearrange("p a c -> p (a c)").bitcast(I32), 0)
+        nc.vector.memset(w2_rows[:].bitcast(I32), 0)
         nc.vector.memset(one[:], 1.0)
-        nc.vector.memset(v_plane[:].bitcast(I32), 0)
-        nc.gpsimd.memset(w3_plane[:].bitcast(I32), 0)
+        nc.vector.memset(planes[:].bitcast(I32), 0)
         nc.scalar.activation(warm[:], one[:], ACT.Abs_reciprocal_sqrt)
 
         w1_codes = [keep.tile([P, H], U32, name=f"w1_codes{a}", align_bytes=64) for a in range(PASSES)]
@@ -86,40 +86,37 @@ def tile_list_lidar_radar_resonance_kernel(
 
         nc.sync.dma_start(offsets[:], offs)
         load_w1(0)
+        nc.sync.dma_start(centre[:], centres.rearrange("(p t) -> p t", t=PACK))
         nc.sync.dma_start(
             tab_rows[0:P:ROW_STEP, :].bitcast(I32),
             tab_scales.bitcast(I32).rearrange("a q t -> q a t"),
         )
-        for r in range(4):
-            nc.sync.dma_start(
-                w2_plane_raw[r:P:32, :, :].bitcast(I32),
-                w2_scales[:, r:16:4, :].rearrange("a q c -> q a c").bitcast(I32),
-            )
+        nc.sync.dma_start(w2_rows[0:P:ROW_STEP, :].bitcast(I32), w2_scales.bitcast(I32).rearrange("a q c -> q a c"))
+        nc.sync.dma_start(
+            rows[0:P:ROW_STEP, S + H : ROW].bitcast(I32),
+            w3_scales[0].bitcast(I32).rearrange("q (a c) -> (q a) c", a=PASSES),
+        )
         load_w1(1)
         tab[0] = relay.tile([P, T], U32, name="tab0", offset=0, align_bytes=64)
         load_tab(0)
-        nc.gpsimd.dma_start(centre[:], centres.rearrange("(p t) -> p t", t=PACK))
-        for r in range(4):
-            nc.gpsimd.dma_start(w3_plane[r:P:32, :].bitcast(I32), w3_scales[0, r:16:4, :].bitcast(I32))
 
         v_rows = keep.tile([P, S], U8, name="v_rows", align_bytes=64)
         nc.vector.tensor_copy(v_rows[:], tab_rows[:].indirect(offsets[:]))
+        nc.vector.tensor_copy(
+            rows[:, S : S + H].rearrange("p (t m) -> p t m", t=PACK), w2_rows[:].rearrange("p (m t) -> p t m", t=PACK)
+        )
+        nc.vector.tensor_copy(rows[:, 0:S].bitcast(I32), v_rows[:].bitcast(I32))
         for q in range(4):
             nc.sync.dma_start(
-                v_plane[32 * q : 32 * q + 4, :].bitcast(I32), v_rows[32 * q : 32 * (q + 1) : ROW_STEP, :].bitcast(I32)
+                planes[32 * q : 32 * q + 4, :].bitcast(I32), rows[32 * q : 32 * (q + 1) : ROW_STEP, :].bitcast(I32)
             )
-        tab[1] = keep.tile([P, T], U32, name="tab1", tag="tab_rows", align_bytes=64)
+        tab[1] = keep.tile([P, T], U32, name="tab1", tag="v_rows", align_bytes=64)
         load_tab(1)
-        w2_raw = keep.tile([P, PASSES, 2 * H], U8, name="w2_raw", tag="v_rows", align_bytes=64)
+        w2_raw = keep.tile([P, PASSES, 2 * H], U8, name="w2_raw", tag="rows", align_bytes=64)
         nc.sync.dma_start(w2_raw[:].bitcast(I32), w2_words.rearrange("a p b -> p a b").bitcast(I32))
 
         w2_codes = keep.tile([P, PASSES, 2 * H], U8, name="w2_codes", align_bytes=64)
-        w2_plane = keep.tile([P, PASSES, H], U8, name="w2_plane", align_bytes=64)
         quantise_w1(0)
-        nc.vector.tensor_copy(
-            w2_plane[:].rearrange("p a (t m) -> p a t m", t=PACK),
-            w2_plane_raw[:].rearrange("p a (m t) -> p a t m", t=PACK),
-        )
         quantise_w1(1)
         gather_words(0, 1)
         gather_words(0, 0)
@@ -160,7 +157,7 @@ def tile_list_lidar_radar_resonance_kernel(
                 lhsT=w1_codes[a][:, P * t : P * (t + 1)].bitcast(E4M3),
                 lhsT_scale=w1_plane[a][:, P * t : P * (t + 1)],
                 rhs=v_codes[a, s][:, c0 - s * HALF : c1 - s * HALF].bitcast(E4M3),
-                rhs_scale=v_plane[:, a * S + c0 : a * S + c1],
+                rhs_scale=planes[:, a * ROW + c0 : a * ROW + c1],
                 start=(a == 0),
                 stop=(a == PASSES - 1),
             )
@@ -169,9 +166,9 @@ def tile_list_lidar_radar_resonance_kernel(
             nc.tensor.matmul_mx(
                 amp[s, t][:],
                 lhsT=w2_codes[:, a, 2 * P * t : 2 * P * (t + 1)].bitcast(E2M1),
-                lhsT_scale=w2_plane[:, a, P * t : P * (t + 1)],
+                lhsT_scale=planes[:, a * ROW + S + P * t : a * ROW + S + P * (t + 1)],
                 rhs=v_codes[a, s][:].bitcast(E4M3),
-                rhs_scale=v_plane[:, a * S + s * HALF : a * S + (s + 1) * HALF],
+                rhs_scale=planes[:, a * ROW + s * HALF : a * ROW + (s + 1) * HALF],
                 start=(a == 0),
                 stop=(a == PASSES - 1),
             )
@@ -269,10 +266,11 @@ def tile_list_lidar_radar_resonance_kernel(
             match[c, i] = psum.tile([P, 2, WIDEST], F32, name=f"front{(2 + (PAIRS * c + i) % 2) if c < 2 else (PAIRS * c + i) % 4}")
             for e in range(2):
                 n0 = P * (2 * i + e)
+                plane0 = (n0 // (N // PASSES)) * ROW + S + H + n0 % (N // PASSES)
                 nc.tensor.matmul_mx(
                     match[c, i][:, e, 0 : c1 - c0],
                     lhsT=w3_codes[:, n0 : n0 + P].bitcast(E4M3),
-                    lhsT_scale=w3_plane[:, n0 : n0 + P],
+                    lhsT_scale=planes[:, plane0 : plane0 + P],
                     rhs=h_codes[:, c0:c1].bitcast(E4M3),
                     rhs_scale=h_plane[:, c0:c1],
                     start=True,

@@ -20,12 +20,12 @@ P = 128
 PACK = 4
 PASSES = K // (P * PACK)
 HALF = 512
-CHUNKS = [(0, 256), (256, 512), (512, 768), (768, 1024)]
+CHUNKS = [(0, 256), (256, 512), (512, 768), (768, 896), (896, 1024)]
 WIDEST = 256
 H_STORES = [(0, 256), (256, 512), (512, 768), (768, 1024)]
 Y_STORES = [(0, 256), (256, 512), (512, 768), (768, 1024)]
-VECTOR_SQUARES = (0,)
-SCALAR_ROUNDS = (2, 3)
+VECTOR_SQUARES = ((0, 0), (0, 1))
+SCALAR_ROUNDS = (2, 3, 4)
 GPSIMD_ROUNDS = ()
 PAIRS = N // (2 * P)
 ROW_STEP = 4
@@ -217,7 +217,7 @@ def tile_list_lidar_radar_resonance_kernel(
             width = CHUNKS[c][1] - CHUNKS[c][0]
             for u in range(2):
                 resp[c, u] = work.tile([P, 2, width], F32, name=f"resp{u}")
-                if c in VECTOR_SQUARES:
+                if (c, u) in VECTOR_SQUARES:
                     nc.vector.tensor_tensor(resp[c, u][:], root[c, u][:], root[c, u][:], ALU.mult)
                 else:
                     nc.scalar.activation(resp[c, u][:], root[c, u][:], ACT.Square)
@@ -263,7 +263,7 @@ def tile_list_lidar_radar_resonance_kernel(
 
         def score(c, i):
             c0, c1 = CHUNKS[c]
-            match[c, i] = psum.tile([P, 2, WIDEST], F32, name=f"front{(2 + (PAIRS * c + i) % 2) if c < 2 else (PAIRS * c + i) % 4}")
+            match[c, i] = psum.tile([P, 2, WIDEST], F32, name=f"front{(2 + (PAIRS * c + i) % 2) if c < 3 else (PAIRS * c + i) % 4}")
             for e in range(2):
                 n0 = P * (2 * i + e)
                 plane0 = (n0 // (N // PASSES)) * ROW + S + H + n0 % (N // PASSES)

@@ -47,7 +47,7 @@ def tile_list_lidar_radar_resonance_kernel(
         tab_rows = keep.tile([P, T], U8, name="tab_rows", align_bytes=64)
         w2_rows = keep.tile([P, H], U8, name="w2_rows", align_bytes=64)
         rows = keep.tile([P, ROW], U8, name="rows", align_bytes=64)
-        planes = keep.tile([P, PASSES * ROW], U8, name="planes", align_bytes=64)
+        planes = [keep.tile([P, ROW], U8, name=f"planes{a}", align_bytes=64) for a in range(PASSES)]
         one = keep.tile([P, 1], F32, name="one")
         warm = keep.tile([P, 1], F32, name="warm")
         centre = keep.tile([P, PACK], F32, name="centre")
@@ -55,7 +55,8 @@ def tile_list_lidar_radar_resonance_kernel(
         nc.vector.memset(tab_rows[:].bitcast(I32), 0)
         nc.vector.memset(w2_rows[:].bitcast(I32), 0)
         nc.vector.memset(one[:], 1.0)
-        nc.vector.memset(planes[:].bitcast(I32), 0)
+        for a in range(PASSES):
+            nc.vector.memset(planes[a][:].bitcast(I32), 0)
         nc.scalar.activation(warm[:], one[:], ACT.Abs_reciprocal_sqrt)
 
         w1_codes = [keep.tile([P, H], U32, name=f"w1_codes{a}", align_bytes=64) for a in range(PASSES)]
@@ -85,7 +86,7 @@ def tile_list_lidar_radar_resonance_kernel(
             )
 
         nc.sync.dma_start(offsets[:], offs)
-        load_w1(0)
+        load_w1(1)
         nc.sync.dma_start(centre[:], centres.rearrange("(p t) -> p t", t=PACK))
         nc.sync.dma_start(
             tab_rows[0:P:ROW_STEP, :].bitcast(I32),
@@ -96,9 +97,9 @@ def tile_list_lidar_radar_resonance_kernel(
             rows[0:P:ROW_STEP, S + H : ROW].bitcast(I32),
             w3_scales[0].bitcast(I32).rearrange("q (a c) -> (q a) c", a=PASSES),
         )
-        load_w1(1)
         tab[0] = relay.tile([P, T], U32, name="tab0", offset=0, align_bytes=64)
         load_tab(0)
+        load_w1(0)
 
         v_rows = keep.tile([P, S], U8, name="v_rows", align_bytes=64)
         nc.vector.tensor_copy(v_rows[:], tab_rows[:].indirect(offsets[:]))
@@ -106,24 +107,30 @@ def tile_list_lidar_radar_resonance_kernel(
             rows[:, S : S + H].rearrange("p (t m) -> p t m", t=PACK), w2_rows[:].rearrange("p (m t) -> p t m", t=PACK)
         )
         nc.vector.tensor_copy(rows[:, 0:S].bitcast(I32), v_rows[:].bitcast(I32))
-        for q in range(4):
-            nc.sync.dma_start(
-                planes[32 * q : 32 * q + 4, :].bitcast(I32), rows[32 * q : 32 * (q + 1) : ROW_STEP, :].bitcast(I32)
-            )
+
+        def move_rows(a):
+            for r in range(4):
+                nc.sync.dma_start(
+                    planes[a][r:P:32, :].bitcast(I32),
+                    rows[ROW_STEP * (PASSES * r + a) : P : 32, :].bitcast(I32),
+                )
+
+        move_rows(0)
         tab[1] = keep.tile([P, T], U32, name="tab1", tag="v_rows", align_bytes=64)
         load_tab(1)
-        w2_raw = keep.tile([P, PASSES, 2 * H], U8, name="w2_raw", tag="rows", align_bytes=64)
-        nc.sync.dma_start(w2_raw[:].bitcast(I32), w2_words.rearrange("a p b -> p a b").bitcast(I32))
+        move_rows(1)
 
         w2_codes = keep.tile([P, PASSES, 2 * H], U8, name="w2_codes", align_bytes=64)
-        quantise_w1(0)
         quantise_w1(1)
-        gather_words(0, 1)
         gather_words(0, 0)
+        gather_words(0, 1)
+        quantise_w1(0)
 
-        w3_codes = relay.tile([P, N], U32, name="w3_codes", offset=0, align_bytes=64)
+        w2_raw = relay.tile([P, PASSES, 2 * H], U8, name="w2_raw", offset=0, align_bytes=64)
+        nc.sync.dma_start(w2_raw[:].bitcast(I32), w2_words.rearrange("a p b -> p a b").bitcast(I32))
+        w3_codes = relay.tile([P, N], U32, name="w3_codes", offset=4 * H, align_bytes=64)
         nc.sync.dma_start(w3_codes[:].bitcast(I32), w3_words[0].rearrange("p c i -> p (c i)").bitcast(I32))
-        floors = relay.tile([P, PAIRS * 2 * S], F32, name="floors", offset=4 * N, align_bytes=64)
+        floors = relay.tile([P, PAIRS * 2 * S], F32, name="floors", offset=4 * H + 4 * N, align_bytes=64)
         floor = [floors[:, 2 * S * i : 2 * S * (i + 1)].rearrange("p (u j) -> p u j", u=2) for i in range(PAIRS)]
         for i in range(PAIRS):
             nc.sync.dma_start(floor[i], least[2 * P * i : 2 * P * (i + 1), :].rearrange("(u p) j -> p u j", p=P))
@@ -157,7 +164,7 @@ def tile_list_lidar_radar_resonance_kernel(
                 lhsT=w1_codes[a][:, P * t : P * (t + 1)].bitcast(E4M3),
                 lhsT_scale=w1_plane[a][:, P * t : P * (t + 1)],
                 rhs=v_codes[a, s][:, c0 - s * HALF : c1 - s * HALF].bitcast(E4M3),
-                rhs_scale=planes[:, a * ROW + c0 : a * ROW + c1],
+                rhs_scale=planes[a][:, c0:c1],
                 start=(a == 0),
                 stop=(a == PASSES - 1),
             )
@@ -166,9 +173,9 @@ def tile_list_lidar_radar_resonance_kernel(
             nc.tensor.matmul_mx(
                 amp[s, t][:],
                 lhsT=w2_codes[:, a, 2 * P * t : 2 * P * (t + 1)].bitcast(E2M1),
-                lhsT_scale=planes[:, a * ROW + S + P * t : a * ROW + S + P * (t + 1)],
+                lhsT_scale=planes[a][:, S + P * t : S + P * (t + 1)],
                 rhs=v_codes[a, s][:].bitcast(E4M3),
-                rhs_scale=planes[:, a * ROW + s * HALF : a * ROW + (s + 1) * HALF],
+                rhs_scale=planes[a][:, s * HALF : (s + 1) * HALF],
                 start=(a == 0),
                 stop=(a == PASSES - 1),
             )
@@ -266,11 +273,11 @@ def tile_list_lidar_radar_resonance_kernel(
             match[c, i] = psum.tile([P, 2, WIDEST], F32, name=f"front{(2 + (PAIRS * c + i) % 2) if c < 3 else (PAIRS * c + i) % 4}")
             for e in range(2):
                 n0 = P * (2 * i + e)
-                plane0 = (n0 // (N // PASSES)) * ROW + S + H + n0 % (N // PASSES)
+                plane0 = S + H + n0 % (N // PASSES)
                 nc.tensor.matmul_mx(
                     match[c, i][:, e, 0 : c1 - c0],
                     lhsT=w3_codes[:, n0 : n0 + P].bitcast(E4M3),
-                    lhsT_scale=planes[:, plane0 : plane0 + P],
+                    lhsT_scale=planes[n0 // (N // PASSES)][:, plane0 : plane0 + P],
                     rhs=h_codes[:, c0:c1].bitcast(E4M3),
                     rhs_scale=h_plane[:, c0:c1],
                     start=True,

@@ -20,13 +20,9 @@ P = 128
 PACK = 4
 PASSES = K // (P * PACK)
 HALF = 512
-CHUNKS = [(0, 256), (256, 512), (512, 768), (768, 896), (896, 1024)]
-WIDEST = 256
-H_STORES = [(0, 256), (256, 512), (512, 768), (768, 1024)]
-Y_STORES = [(0, 256), (256, 512), (512, 768), (768, 1024)]
-VECTOR_SQUARES = ((0, 0), (0, 1))
-SCALAR_ROUNDS = (2, 3, 4)
-GPSIMD_ROUNDS = ()
+HALVES = S // HALF
+QUARTER = HALF // 2
+TILES = N // P
 PAIRS = N // (2 * P)
 ROW_STEP = 4
 ROW = S + H + N // PASSES
@@ -142,12 +138,11 @@ def tile_list_lidar_radar_resonance_kernel(
         )
         gather_words(1, 1)
 
-        h_tiles = [keep.tile([P, PACK, HALF], F32, name=f"h{s}") for s in range(S // HALF)]
-        y_tiles = {(s, i): keep.tile([P, 2, HALF], F32, name=f"y{s}_{i}") for s in range(S // HALF) for i in range(PAIRS)}
+        h_all = [keep.tile([P, PACK, HALF], F32, name=f"h{s}") for s in range(HALVES)]
+        y_tiles = {(s, i): keep.tile([P, HALF], F32, name=f"y{s}_{i}") for s in range(HALVES) for i in range(TILES)}
         h_codes = keep.tile([P, S], U32, name="h_codes", align_bytes=64)
         h_plane = keep.tile([P, S], U8, name="h_plane", align_bytes=64)
         out_1_rows = out_1.rearrange("(p t) j -> p t j", t=PACK)
-        out_0_rows = out_0.rearrange("(i p) j -> p i j", p=P)
         out_2_words = out_2[0].rearrange("p m t -> p (m t)").bitcast(I32)
 
         pos = {}
@@ -157,172 +152,124 @@ def tile_list_lidar_radar_resonance_kernel(
         h_bf = {}
         match = {}
 
-        def pos_pass(out, a, t, c0, c1):
-            s = c0 // HALF
+        def cols(s):
+            return slice(s * HALF, (s + 1) * HALF)
+
+        def pos_pass(a, s, t):
             nc.tensor.matmul_mx(
-                out,
+                pos[s, t][:],
                 lhsT=w1_codes[a][:, P * t : P * (t + 1)].bitcast(E4M3),
                 lhsT_scale=w1_plane[a][:, P * t : P * (t + 1)],
-                rhs=v_codes[a, s][:, c0 - s * HALF : c1 - s * HALF].bitcast(E4M3),
-                rhs_scale=planes[a][:, c0:c1],
+                rhs=v_codes[a, s][:].bitcast(E4M3),
+                rhs_scale=planes[a][:, cols(s)],
                 start=(a == 0),
                 stop=(a == PASSES - 1),
             )
 
-        def amp_pass(a, t, s):
+        def amp_pass(a, s, t):
             nc.tensor.matmul_mx(
                 amp[s, t][:],
                 lhsT=w2_codes[:, a, 2 * P * t : 2 * P * (t + 1)].bitcast(E2M1),
                 lhsT_scale=planes[a][:, S + P * t : S + P * (t + 1)],
                 rhs=v_codes[a, s][:].bitcast(E4M3),
-                rhs_scale=planes[a][:, s * HALF : (s + 1) * HALF],
+                rhs_scale=planes[a][:, cols(s)],
                 start=(a == 0),
                 stop=(a == PASSES - 1),
             )
 
-        def first_half_products():
-            banks = [psum.tile([P, HALF], F32, name=f"front{t}") for t in range(PACK)]
-            for t in range(PACK):
-                amp[0, t] = psum.tile([P, HALF], F32, name=f"amp{t}")
-                for c, (c0, c1) in enumerate(CHUNKS):
-                    if c1 <= HALF:
-                        pos[c, t] = banks[t][:, c0:c1]
+        def positions(s, t):
+            pos[s, t] = psum.tile([P, HALF], F32, name=f"front{t}")
             for a in range(PASSES):
-                for t in range(PACK):
-                    pos_pass(banks[t][:], a, t, 0, HALF)
-            for t in range(PACK):
-                for a in range(PASSES):
-                    amp_pass(a, t, 0)
+                pos_pass(a, s, t)
 
-        def second_half_amp():
-            for t in range(PACK):
-                amp[1, t] = psum.tile([P, HALF], F32, name=f"amp{t}")
-                for a in range(PASSES):
-                    amp_pass(a, t, 1)
+        def amplitudes(s, t):
+            amp[s, t] = psum.tile([P, HALF], F32, name=f"amp{t}")
+            for a in range(PASSES):
+                amp_pass(a, s, t)
 
-        def chunk_pos(c):
-            c0, c1 = CHUNKS[c]
-            for u in range(2):
-                bank = psum.tile([P, 2, WIDEST], F32, name=f"front{u}")
-                for e in range(2):
-                    pos[c, 2 * u + e] = bank[:, e, 0 : c1 - c0]
-                    for a in range(PASSES):
-                        pos_pass(pos[c, 2 * u + e], a, 2 * u + e, c0, c1)
+        def roots(s, t):
+            square = work.tile([P, HALF], F32, name="square")
+            nc.scalar.activation(square[:], pos[s, t][:], ACT.Square, bias=centre[:, t : t + 1], scale=-1.0)
+            root[s, t] = work.tile([P, HALF], F32, name="root", bufs=3)
+            nc.scalar.activation(root[s, t][:], square[:], ACT.Abs_reciprocal_sqrt, bias=one[:])
 
-        def roots(c):
-            width = CHUNKS[c][1] - CHUNKS[c][0]
-            square = [work.tile([P, 2, width], F32, name=f"square{u}") for u in range(2)]
-            for t in range(PACK):
-                nc.scalar.activation(
-                    square[t // 2][:, t % 2, :], pos[c, t], ACT.Square, bias=centre[:, t : t + 1], scale=-1.0
-                )
-            for u in range(2):
-                root[c, u] = work.tile([P, 2, width], F32, name=f"root{u}")
-                nc.scalar.activation(root[c, u][:], square[u][:], ACT.Abs_reciprocal_sqrt, bias=one[:])
-
-        def responses(c):
-            width = CHUNKS[c][1] - CHUNKS[c][0]
-            for u in range(2):
-                resp[c, u] = work.tile([P, 2, width], F32, name=f"resp{u}")
-                if (c, u) in VECTOR_SQUARES:
-                    nc.vector.tensor_tensor(resp[c, u][:], root[c, u][:], root[c, u][:], ALU.mult)
-                else:
-                    nc.scalar.activation(resp[c, u][:], root[c, u][:], ACT.Square)
-
-        def half_cols(c):
-            c0, c1 = CHUNKS[c]
-            return slice(c0 % HALF, c0 % HALF + c1 - c0)
-
-        def amplify(c):
-            c0, c1 = CHUNKS[c]
-            s = c0 // HALF
-            for t in range(PACK):
-                nc.vector.tensor_tensor(
-                    h_tiles[s][:, t, half_cols(c)], amp[s, t][:, half_cols(c)], resp[c, t // 2][:, t % 2, :], ALU.mult
-                )
-            for j0, j1 in H_STORES:
-                if j1 == c1:
-                    nc.sync.dma_start(out_1_rows[:, :, j0:j1], h_tiles[s][:, :, j0 - s * HALF : j1 - s * HALF])
-
-        def round_h(c):
-            c0, c1 = CHUNKS[c]
-            h_bf[c] = work.tile([P, PACK * (c1 - c0)], BF16, name="h_bf", align_bytes=64)
-            source = h_tiles[c0 // HALF][:, :, half_cols(c)]
-            if c in GPSIMD_ROUNDS:
-                nc.gpsimd.tensor_scalar(
-                    h_bf[c][:].rearrange("p (c t) -> p c t", t=PACK), source.rearrange("p t c -> p c t"),
-                    1.0, 0.0, ALU.mult, ALU.add,
-                )
+        def response(s, t):
+            resp[s, t] = work.tile([P, HALF], F32, name="resp", bufs=4)
+            if s == 0:
+                nc.vector.tensor_tensor(resp[s, t][:], root[s, t][:], root[s, t][:], ALU.mult)
             else:
-                (nc.scalar.copy if c in SCALAR_ROUNDS else nc.vector.tensor_copy)(
-                    h_bf[c][:].rearrange("p (c i t) -> p c t i", t=PACK, i=4),
-                    source.rearrange("p t (c i) -> p c t i", i=4),
-                )
+                nc.scalar.activation(resp[s, t][:], root[s, t][:], ACT.Square)
 
-        def quantise(c):
-            c0, c1 = CHUNKS[c]
-            nc.vector.quantize_mx(h_codes[:, c0:c1].bitcast(E4M3), h_plane[:, c0:c1], h_bf[c][:])
-            if c1 % HALF == 0:
-                nc.sync.dma_start(out_2_words[:, c1 - HALF : c1], h_codes[:, c1 - HALF : c1].bitcast(I32))
-            if c1 == S:
+        def amplify(s, t):
+            nc.vector.tensor_tensor(h_all[s][:, t, :], amp[s, t][:], resp[s, t][:], ALU.mult)
+            if t % 2 == 1:
+                nc.sync.dma_start(out_1_rows[:, t - 1 : t + 1, cols(s)], h_all[s][:, t - 1 : t + 1, :])
+
+        def round_h(s, e, copy):
+            h_bf[s, e] = keep.tile([P, PACK * QUARTER], BF16, name=f"h_bf{s}_{e}", align_bytes=64)
+            copy(
+                h_bf[s, e][:].rearrange("p (c i t) -> p c t i", t=PACK, i=4),
+                h_all[s][:, :, e * QUARTER : (e + 1) * QUARTER].rearrange("p t (c i) -> p c t i", i=4),
+            )
+
+        def quantise(s, e):
+            c0 = s * HALF + e * QUARTER
+            nc.vector.quantize_mx(h_codes[:, c0 : c0 + QUARTER].bitcast(E4M3), h_plane[:, c0 : c0 + QUARTER], h_bf[s, e][:])
+
+        def store_codes(s):
+            nc.sync.dma_start(out_2_words[:, cols(s)], h_codes[:, cols(s)].bitcast(I32))
+            if s == HALVES - 1:
                 for r in range(4):
                     nc.scalar.dma_start(out_3[0, r:16:4, :].bitcast(I32), h_plane[r:P:32, :].bitcast(I32))
 
-        def score(c, i):
-            c0, c1 = CHUNKS[c]
-            match[c, i] = psum.tile([P, 2, WIDEST], F32, name=f"front{(2 + (PAIRS * c + i) % 2) if c < 3 else (PAIRS * c + i) % 4}")
-            for e in range(2):
-                n0 = P * (2 * i + e)
-                plane0 = S + H + n0 % (N // PASSES)
-                nc.tensor.matmul_mx(
-                    match[c, i][:, e, 0 : c1 - c0],
-                    lhsT=w3_codes[:, n0 : n0 + P].bitcast(E4M3),
-                    lhsT_scale=planes[n0 // (N // PASSES)][:, plane0 : plane0 + P],
-                    rhs=h_codes[:, c0:c1].bitcast(E4M3),
-                    rhs_scale=h_plane[:, c0:c1],
-                    start=True,
-                    stop=True,
-                )
-
-        def keep_above(c, i):
-            c0, c1 = CHUNKS[c]
-            s = c0 // HALF
-            nc.vector.tensor_tensor(
-                y_tiles[s, i][:, :, half_cols(c)], match[c, i][:, :, 0 : c1 - c0], floor[i][:, :, c0:c1], ALU.max
+        def score(s, i, bank):
+            match[s, i] = psum.tile([P, HALF], F32, name=bank)
+            n0 = P * i
+            plane0 = S + H + n0 % (N // PASSES)
+            nc.tensor.matmul_mx(
+                match[s, i][:],
+                lhsT=w3_codes[:, n0 : n0 + P].bitcast(E4M3),
+                lhsT_scale=planes[n0 // (N // PASSES)][:, plane0 : plane0 + P],
+                rhs=h_codes[:, cols(s)].bitcast(E4M3),
+                rhs_scale=h_plane[:, cols(s)],
+                start=True,
+                stop=True,
             )
-            for j0, j1 in Y_STORES:
-                if j1 == c1:
-                    nc.sync.dma_start(
-                        out_0_rows[:, 2 * i : 2 * i + 2, j0:j1], y_tiles[s, i][:, :, j0 - s * HALF : j1 - s * HALF]
-                    )
 
-        first_half_products()
-        roots(0)
-        responses(0)
-        roots(1)
-        responses(1)
-        amplify(0)
-        round_h(0)
-        quantise(0)
-        chunk_pos(2)
-        for c in range(len(CHUNKS)):
-            more = c + 1 < len(CHUNKS)
-            score(c, 0)
-            score(c, 1)
-            if c + 2 < len(CHUNKS):
-                roots(c + 2)
-                responses(c + 2)
-            if c + 3 < len(CHUNKS):
-                chunk_pos(c + 3)
-            if more:
-                amplify(c + 1)
-            if c == 0:
-                second_half_amp()
-            keep_above(c, 0)
-            score(c, 2)
-            if more:
-                round_h(c + 1)
-            keep_above(c, 1)
-            if more:
-                quantise(c + 1)
-            keep_above(c, 2)
+        def keep_above(s, i):
+            nc.vector.tensor_tensor(y_tiles[s, i][:], match[s, i][:], floor[i // 2][:, i % 2, cols(s)], ALU.max)
+            nc.sync.dma_start(out_0[P * i : P * (i + 1), cols(s)], y_tiles[s, i][:])
+
+        for t in range(PACK):
+            pos[0, t] = psum.tile([P, HALF], F32, name=f"front{t}")
+        for a in range(PASSES):
+            for t in range(PACK):
+                pos_pass(a, 0, t)
+        for t in range(PACK):
+            amplitudes(0, t)
+        for t in range(PACK):
+            roots(0, t)
+            positions(1, t)
+            response(0, t)
+            amplify(0, t)
+            amplitudes(1, t)
+        for e in range(2):
+            round_h(0, e, nc.vector.tensor_copy)
+        for e in range(2):
+            quantise(0, e)
+        store_codes(0)
+        for t in range(PACK):
+            roots(1, t)
+            response(1, t)
+            amplify(1, t)
+        round_h(1, 0, nc.scalar.copy)
+        round_h(1, 1, nc.vector.tensor_copy)
+        for i in range(TILES):
+            score(0, i, f"front{i % 3}")
+            keep_above(0, i)
+        quantise(1, 1)
+        quantise(1, 0)
+        store_codes(1)
+        for i in range(TILES):
+            score(1, i, f"amp{i % PACK}")
+            keep_above(1, i)

@@ -23,6 +23,8 @@ HALF = 512
 HALVES = S // HALF
 QUARTER = HALF // 2
 TILES = N // P
+FILL = 2
+QUARTER_ORDER = ((0, 1), (1, 0))
 PAIRS = N // (2 * P)
 ROW_STEP = 4
 ROW = S + H + N // PASSES
@@ -202,7 +204,9 @@ def tile_list_lidar_radar_resonance_kernel(
 
         def amplify(s, t):
             nc.vector.tensor_tensor(h_all[s][:, t, :], amp[s, t][:], resp[s, t][:], ALU.mult)
-            if t % 2 == 1:
+            if s == 1:
+                nc.sync.dma_start(out_1_rows[:, t, cols(s)], h_all[s][:, t, :])
+            elif t % 2 == 1:
                 nc.sync.dma_start(out_1_rows[:, t - 1 : t + 1, cols(s)], h_all[s][:, t - 1 : t + 1, :])
 
         def round_h(s, e, copy):
@@ -226,15 +230,17 @@ def tile_list_lidar_radar_resonance_kernel(
             match[s, i] = psum.tile([P, HALF], F32, name=bank)
             n0 = P * i
             plane0 = S + H + n0 % (N // PASSES)
-            nc.tensor.matmul_mx(
-                match[s, i][:],
-                lhsT=w3_codes[:, n0 : n0 + P].bitcast(E4M3),
-                lhsT_scale=planes[n0 // (N // PASSES)][:, plane0 : plane0 + P],
-                rhs=h_codes[:, cols(s)].bitcast(E4M3),
-                rhs_scale=h_plane[:, cols(s)],
-                start=True,
-                stop=True,
-            )
+            for e in QUARTER_ORDER[s]:
+                c0 = s * HALF + e * QUARTER
+                nc.tensor.matmul_mx(
+                    match[s, i][:, e * QUARTER : (e + 1) * QUARTER],
+                    lhsT=w3_codes[:, n0 : n0 + P].bitcast(E4M3),
+                    lhsT_scale=planes[n0 // (N // PASSES)][:, plane0 : plane0 + P],
+                    rhs=h_codes[:, c0 : c0 + QUARTER].bitcast(E4M3),
+                    rhs_scale=h_plane[:, c0 : c0 + QUARTER],
+                    start=True,
+                    stop=True,
+                )
 
         def keep_above(s, i):
             nc.vector.tensor_tensor(y_tiles[s, i][:], match[s, i][:], floor[i // 2][:, i % 2, cols(s)], ALU.max)
@@ -264,12 +270,15 @@ def tile_list_lidar_radar_resonance_kernel(
             amplify(1, t)
         round_h(1, 0, nc.scalar.copy)
         round_h(1, 1, nc.vector.tensor_copy)
-        for i in range(TILES):
+        for i in range(TILES - FILL):
             score(0, i, f"front{i % 3}")
             keep_above(0, i)
         quantise(1, 1)
         quantise(1, 0)
         store_codes(1)
+        for i in range(TILES - FILL, TILES):
+            score(0, i, f"front{i % 3}")
+            keep_above(0, i)
         for i in range(TILES):
             score(1, i, f"amp{i % PACK}")
             keep_above(1, i)

@@ -25,9 +25,10 @@ QUARTER = HALF // 2
 TILES = N // P
 FILL = 2
 QUARTER_ORDER = ((0, 1), (1, 0))
+Y_STORES = (((0, 2), (2, 4), (4, 6)), tuple((i, i + 1) for i in range(TILES)))
 PAIRS = N // (2 * P)
 ROW_STEP = 4
-ROW = S + H + N // PASSES
+ROW = S + PASSES * H + N
 
 
 def tile_list_lidar_radar_resonance_kernel(
@@ -43,9 +44,10 @@ def tile_list_lidar_radar_resonance_kernel(
 
         offsets = keep.tile([P, S // 16], U16, name="offsets")
         tab_rows = keep.tile([P, T], U8, name="tab_rows", align_bytes=64)
-        w2_rows = keep.tile([P, H], U8, name="w2_rows", align_bytes=64)
+        w2_rows = keep.tile([P, PASSES * H], U8, name="w2_rows", align_bytes=64)
         rows = keep.tile([P, ROW], U8, name="rows", align_bytes=64)
-        planes = [keep.tile([P, ROW], U8, name=f"planes{a}", align_bytes=64) for a in range(PASSES)]
+        widths = (S, ROW)
+        planes = [keep.tile([P, widths[a]], U8, name=f"planes{a}", align_bytes=64) for a in range(PASSES)]
         one = keep.tile([P, 1], F32, name="one")
         warm = keep.tile([P, 1], F32, name="warm")
         centre = keep.tile([P, PACK], F32, name="centre")
@@ -90,11 +92,12 @@ def tile_list_lidar_radar_resonance_kernel(
             tab_rows[0:P:ROW_STEP, :].bitcast(I32),
             tab_scales.bitcast(I32).rearrange("a q t -> q a t"),
         )
-        nc.sync.dma_start(w2_rows[0:P:ROW_STEP, :].bitcast(I32), w2_scales.bitcast(I32).rearrange("a q c -> q a c"))
+        last_pass_rows = slice(ROW_STEP, P, PASSES * ROW_STEP)
         nc.sync.dma_start(
-            rows[0:P:ROW_STEP, S + H : ROW].bitcast(I32),
-            w3_scales[0].bitcast(I32).rearrange("q (a c) -> (q a) c", a=PASSES),
+            w2_rows[last_pass_rows, :].bitcast(I32).rearrange("q (a c) -> q a c", a=PASSES),
+            w2_scales.bitcast(I32).rearrange("a q c -> q a c"),
         )
+        nc.sync.dma_start(rows[last_pass_rows, S + PASSES * H : ROW].bitcast(I32), w3_scales[0].bitcast(I32))
         tab[0] = relay.tile([P, T], U32, name="tab0", offset=0, align_bytes=64)
         load_tab(0)
         load_w1(0)
@@ -102,7 +105,8 @@ def tile_list_lidar_radar_resonance_kernel(
         v_rows = keep.tile([P, S], U8, name="v_rows", align_bytes=64)
         nc.vector.tensor_copy(v_rows[:], tab_rows[:].indirect(offsets[:]))
         nc.vector.tensor_copy(
-            rows[:, S : S + H].rearrange("p (t m) -> p t m", t=PACK), w2_rows[:].rearrange("p (m t) -> p t m", t=PACK)
+            rows[:, S : S + PASSES * H].rearrange("p (a t m) -> p a t m", a=PASSES, t=PACK),
+            w2_rows[:].rearrange("p (a m t) -> p a t m", a=PASSES, t=PACK),
         )
         nc.vector.tensor_copy(rows[:, 0:S].bitcast(I32), v_rows[:].bitcast(I32))
 
@@ -110,7 +114,7 @@ def tile_list_lidar_radar_resonance_kernel(
             for r in range(4):
                 nc.sync.dma_start(
                     planes[a][r:P:32, :].bitcast(I32),
-                    rows[ROW_STEP * (PASSES * r + a) : P : 32, :].bitcast(I32),
+                    rows[ROW_STEP * (PASSES * r + a) : P : 32, 0 : widths[a]].bitcast(I32),
                 )
 
         move_rows(0)
@@ -141,7 +145,8 @@ def tile_list_lidar_radar_resonance_kernel(
         gather_words(1, 1)
 
         h_all = [keep.tile([P, PACK, HALF], F32, name=f"h{s}") for s in range(HALVES)]
-        y_tiles = {(s, i): keep.tile([P, HALF], F32, name=f"y{s}_{i}") for s in range(HALVES) for i in range(TILES)}
+        y_all = [keep.tile([P, TILES, HALF], F32, name=f"y{s}") for s in range(HALVES)]
+        out_0_rows = out_0.rearrange("(i p) j -> p i j", p=P)
         h_codes = keep.tile([P, S], U32, name="h_codes", align_bytes=64)
         h_plane = keep.tile([P, S], U8, name="h_plane", align_bytes=64)
         out_1_rows = out_1.rearrange("(p t) j -> p t j", t=PACK)
@@ -172,7 +177,7 @@ def tile_list_lidar_radar_resonance_kernel(
             nc.tensor.matmul_mx(
                 amp[s, t][:],
                 lhsT=w2_codes[:, a, 2 * P * t : 2 * P * (t + 1)].bitcast(E2M1),
-                lhsT_scale=planes[a][:, S + P * t : S + P * (t + 1)],
+                lhsT_scale=planes[1][:, S + H * a + P * t : S + H * a + P * (t + 1)],
                 rhs=v_codes[a, s][:].bitcast(E4M3),
                 rhs_scale=planes[a][:, cols(s)],
                 start=(a == 0),
@@ -229,13 +234,13 @@ def tile_list_lidar_radar_resonance_kernel(
         def score(s, i, bank):
             match[s, i] = psum.tile([P, HALF], F32, name=bank)
             n0 = P * i
-            plane0 = S + H + n0 % (N // PASSES)
+            plane0 = S + PASSES * H + n0
             for e in QUARTER_ORDER[s]:
                 c0 = s * HALF + e * QUARTER
                 nc.tensor.matmul_mx(
                     match[s, i][:, e * QUARTER : (e + 1) * QUARTER],
                     lhsT=w3_codes[:, n0 : n0 + P].bitcast(E4M3),
-                    lhsT_scale=planes[n0 // (N // PASSES)][:, plane0 : plane0 + P],
+                    lhsT_scale=planes[1][:, plane0 : plane0 + P],
                     rhs=h_codes[:, c0 : c0 + QUARTER].bitcast(E4M3),
                     rhs_scale=h_plane[:, c0 : c0 + QUARTER],
                     start=True,
@@ -243,8 +248,10 @@ def tile_list_lidar_radar_resonance_kernel(
                 )
 
         def keep_above(s, i):
-            nc.vector.tensor_tensor(y_tiles[s, i][:], match[s, i][:], floor[i // 2][:, i % 2, cols(s)], ALU.max)
-            nc.sync.dma_start(out_0[P * i : P * (i + 1), cols(s)], y_tiles[s, i][:])
+            nc.vector.tensor_tensor(y_all[s][:, i, :], match[s, i][:], floor[i // 2][:, i % 2, cols(s)], ALU.max)
+            for i0, i1 in Y_STORES[s]:
+                if i1 == i + 1:
+                    nc.sync.dma_start(out_0_rows[:, i0:i1, cols(s)], y_all[s][:, i0:i1, :])
 
         for t in range(PACK):
             pos[0, t] = psum.tile([P, HALF], F32, name=f"front{t}")

@@ -25,7 +25,8 @@ QUARTER = HALF // 2
 TILES = N // P
 FILL = 2
 QUARTER_ORDER = ((0, 1), (1, 0))
-Y_STORES = (((0, 2), (2, 4), (4, 6)), tuple((i, i + 1) for i in range(TILES)))
+Y_STORES = (((0, 2), (2, 4), (4, 6)), ((0, 2), (2, 3), (3, 4), (4, 5), (5, 6)))
+SLICE_PAIRS = ((0, 1), (2, 3))
 PAIRS = N // (2 * P)
 ROW_STEP = 4
 ROW = S + PASSES * H + N
@@ -154,6 +155,7 @@ def tile_list_lidar_radar_resonance_kernel(
 
         pos = {}
         amp = {}
+        square = {}
         root = {}
         resp = {}
         h_bf = {}
@@ -194,24 +196,32 @@ def tile_list_lidar_radar_resonance_kernel(
             for a in range(PASSES):
                 amp_pass(a, s, t)
 
-        def roots(s, t):
-            square = work.tile([P, HALF], F32, name="square")
-            nc.scalar.activation(square[:], pos[s, t][:], ACT.Square, bias=centre[:, t : t + 1], scale=-1.0)
-            root[s, t] = work.tile([P, HALF], F32, name="root", bufs=3)
-            nc.scalar.activation(root[s, t][:], square[:], ACT.Abs_reciprocal_sqrt, bias=one[:])
+        def vector_squared_gap(s, t):
+            gap = keep.tile([P, HALF], F32, name="gap")
+            square[s, t] = keep.tile([P, HALF], F32, name="gap_square")
+            nc.vector.tensor_scalar(gap[:], pos[s, t][:], centre[:, t : t + 1], None, ALU.subtract)
+            nc.vector.tensor_tensor(square[s, t][:], gap[:], gap[:], ALU.mult)
+
+        def squared_gap(s, t):
+            if (s, t) in square:
+                return
+            square[s, t] = work.tile([P, HALF], F32, name="square")
+            nc.scalar.activation(square[s, t][:], pos[s, t][:], ACT.Square, bias=centre[:, t : t + 1], scale=-1.0)
+
+        def inverse_root(s, t):
+            root[s, t] = work.tile([P, HALF], F32, name="root", bufs=4)
+            nc.scalar.activation(root[s, t][:], square[s, t][:], ACT.Abs_reciprocal_sqrt, bias=one[:])
 
         def response(s, t):
             resp[s, t] = work.tile([P, HALF], F32, name="resp", bufs=4)
-            if s == 0:
+            if s == 0 and t < PACK - 1:
                 nc.vector.tensor_tensor(resp[s, t][:], root[s, t][:], root[s, t][:], ALU.mult)
             else:
                 nc.scalar.activation(resp[s, t][:], root[s, t][:], ACT.Square)
 
         def amplify(s, t):
             nc.vector.tensor_tensor(h_all[s][:, t, :], amp[s, t][:], resp[s, t][:], ALU.mult)
-            if s == 1:
-                nc.sync.dma_start(out_1_rows[:, t, cols(s)], h_all[s][:, t, :])
-            elif t % 2 == 1:
+            if t % 2 == 1:
                 nc.sync.dma_start(out_1_rows[:, t - 1 : t + 1, cols(s)], h_all[s][:, t - 1 : t + 1, :])
 
         def round_h(s, e, copy):
@@ -260,21 +270,24 @@ def tile_list_lidar_radar_resonance_kernel(
                 pos_pass(a, 0, t)
         for t in range(PACK):
             amplitudes(0, t)
-        for t in range(PACK):
-            roots(0, t)
-            positions(1, t)
-            response(0, t)
-            amplify(0, t)
-            amplitudes(1, t)
+        vector_squared_gap(0, PACK - 1)
+        for pair in SLICE_PAIRS:
+            for step in (squared_gap, inverse_root, response, amplify):
+                for t in pair:
+                    step(0, t)
+            for t in pair:
+                positions(1, t)
+            for t in pair:
+                amplitudes(1, t)
         for e in range(2):
             round_h(0, e, nc.vector.tensor_copy)
         for e in range(2):
             quantise(0, e)
         store_codes(0)
-        for t in range(PACK):
-            roots(1, t)
-            response(1, t)
-            amplify(1, t)
+        for pair in SLICE_PAIRS:
+            for step in (squared_gap, inverse_root, response, amplify):
+                for t in pair:
+                    step(1, t)
         round_h(1, 0, nc.scalar.copy)
         round_h(1, 1, nc.vector.tensor_copy)
         for i in range(TILES - FILL):

@@ -23,7 +23,7 @@ HALF = 512
 HALVES = S // HALF
 QUARTER = HALF // 2
 TILES = N // P
-FILL = 2
+FILL = 3
 QUARTER_ORDER = ((0, 1), (1, 0))
 Y_STORES = (((0, 2), (2, 4), (4, 6)), ((0, 2), (2, 3), (3, 4), (4, 5), (5, 6)))
 SLICE_PAIRS = ((0, 1), (2, 3))
@@ -196,15 +196,7 @@ def tile_list_lidar_radar_resonance_kernel(
             for a in range(PASSES):
                 amp_pass(a, s, t)
 
-        def vector_squared_gap(s, t):
-            gap = keep.tile([P, HALF], F32, name="gap")
-            square[s, t] = keep.tile([P, HALF], F32, name="gap_square")
-            nc.vector.tensor_scalar(gap[:], pos[s, t][:], centre[:, t : t + 1], None, ALU.subtract)
-            nc.vector.tensor_tensor(square[s, t][:], gap[:], gap[:], ALU.mult)
-
         def squared_gap(s, t):
-            if (s, t) in square:
-                return
             square[s, t] = work.tile([P, HALF], F32, name="square")
             nc.scalar.activation(square[s, t][:], pos[s, t][:], ACT.Square, bias=centre[:, t : t + 1], scale=-1.0)
 
@@ -214,7 +206,7 @@ def tile_list_lidar_radar_resonance_kernel(
 
         def response(s, t):
             resp[s, t] = work.tile([P, HALF], F32, name="resp", bufs=4)
-            if s == 0 and t < PACK - 1:
+            if s == 0:
                 nc.vector.tensor_tensor(resp[s, t][:], root[s, t][:], root[s, t][:], ALU.mult)
             else:
                 nc.scalar.activation(resp[s, t][:], root[s, t][:], ACT.Square)
@@ -270,7 +262,6 @@ def tile_list_lidar_radar_resonance_kernel(
                 pos_pass(a, 0, t)
         for t in range(PACK):
             amplitudes(0, t)
-        vector_squared_gap(0, PACK - 1)
         for pair in SLICE_PAIRS:
             for step in (squared_gap, inverse_root, response, amplify):
                 for t in pair:
@@ -297,8 +288,8 @@ def tile_list_lidar_radar_resonance_kernel(
         quantise(1, 0)
         store_codes(1)
         for i in range(TILES - FILL, TILES):
-            score(0, i, f"front{i % 3}")
+            score(0, i, f"amp{i - TILES + PACK}")
             keep_above(0, i)
         for i in range(TILES):
-            score(1, i, f"amp{i % PACK}")
+            score(1, i, f"front{i % PACK}")
             keep_above(1, i)

@@ -27,7 +27,6 @@ FILL = 3
 QUARTER_ORDER = ((0, 1), (1, 0))
 Y_STORES = (((0, 2), (2, 4), (4, 6)), ((0, 2), (2, 3), (3, 4), (4, 5), (5, 6)))
 SLICE_PAIRS = ((0, 1), (2, 3))
-PAIRS = N // (2 * P)
 ROW_STEP = 4
 ROW = S + PASSES * H + N
 
@@ -45,7 +44,7 @@ def tile_list_lidar_radar_resonance_kernel(
 
         offsets = keep.tile([P, S // 16], U16, name="offsets")
         tab_rows = keep.tile([P, T], U8, name="tab_rows", align_bytes=64)
-        w2_rows = keep.tile([P, PASSES * H], U8, name="w2_rows", align_bytes=64)
+        w2_rows = keep.tile([P, PASSES * H + N], U8, name="w2_rows", align_bytes=64)
         rows = keep.tile([P, ROW], U8, name="rows", align_bytes=64)
         widths = (S, ROW)
         planes = [keep.tile([P, widths[a]], U8, name=f"planes{a}", align_bytes=64) for a in range(PASSES)]
@@ -95,21 +94,25 @@ def tile_list_lidar_radar_resonance_kernel(
         )
         last_pass_rows = slice(ROW_STEP, P, PASSES * ROW_STEP)
         nc.sync.dma_start(
-            w2_rows[last_pass_rows, :].bitcast(I32).rearrange("q (a c) -> q a c", a=PASSES),
+            w2_rows[last_pass_rows, 0 : PASSES * H].bitcast(I32).rearrange("q (a c) -> q a c", a=PASSES),
             w2_scales.bitcast(I32).rearrange("a q c -> q a c"),
         )
-        nc.sync.dma_start(rows[last_pass_rows, S + PASSES * H : ROW].bitcast(I32), w3_scales[0].bitcast(I32))
+        nc.sync.dma_start(w2_rows[last_pass_rows, PASSES * H :].bitcast(I32), w3_scales[0].bitcast(I32))
         tab[0] = relay.tile([P, T], U32, name="tab0", offset=0, align_bytes=64)
         load_tab(0)
         load_w1(0)
 
         v_rows = keep.tile([P, S], U8, name="v_rows", align_bytes=64)
         nc.vector.tensor_copy(v_rows[:], tab_rows[:].indirect(offsets[:]))
+        nc.vector.tensor_copy(rows[:, 0:S].bitcast(I32), v_rows[:].bitcast(I32))
         nc.vector.tensor_copy(
             rows[:, S : S + PASSES * H].rearrange("p (a t m) -> p a t m", a=PASSES, t=PACK),
-            w2_rows[:].rearrange("p (a m t) -> p a t m", a=PASSES, t=PACK),
+            w2_rows[:, 0 : PASSES * H].rearrange("p (a m t) -> p a t m", a=PASSES, t=PACK),
         )
-        nc.vector.tensor_copy(rows[:, 0:S].bitcast(I32), v_rows[:].bitcast(I32))
+        nc.vector.tensor_copy(
+            rows[:, S + PASSES * H : ROW].rearrange("p (i m) -> p i m", i=TILES),
+            w2_rows[:, PASSES * H :].rearrange("p (m i) -> p i m", i=TILES),
+        )
 
         def move_rows(a):
             for r in range(4):
@@ -131,12 +134,10 @@ def tile_list_lidar_radar_resonance_kernel(
 
         w2_raw = relay.tile([P, PASSES, 2 * H], U8, name="w2_raw", offset=0, align_bytes=64)
         nc.sync.dma_start(w2_raw[:].bitcast(I32), w2_words.rearrange("a p b -> p a b").bitcast(I32))
-        w3_codes = relay.tile([P, N], U32, name="w3_codes", offset=4 * H, align_bytes=64)
-        nc.sync.dma_start(w3_codes[:].bitcast(I32), w3_words[0].rearrange("p c i -> p (c i)").bitcast(I32))
-        floors = relay.tile([P, PAIRS * 2 * S], F32, name="floors", offset=4 * H + 4 * N, align_bytes=64)
-        floor = [floors[:, 2 * S * i : 2 * S * (i + 1)].rearrange("p (u j) -> p u j", u=2) for i in range(PAIRS)]
-        for i in range(PAIRS):
-            nc.sync.dma_start(floor[i], least[2 * P * i : 2 * P * (i + 1), :].rearrange("(u p) j -> p u j", p=P))
+        w3_raw = relay.tile([P, N], U32, name="w3_raw", offset=4 * H, align_bytes=64)
+        nc.sync.dma_start(w3_raw[:].bitcast(I32), w3_words[0].rearrange("p c i -> p (c i)").bitcast(I32))
+        floor = relay.tile([P, TILES, S], F32, name="floor", offset=4 * H + 4 * N, align_bytes=64)
+        nc.sync.dma_start(floor[:], least.rearrange("(p i) j -> p i j", i=TILES))
 
         gather_words(1, 0)
         nc.vector.tensor_copy(
@@ -144,10 +145,16 @@ def tile_list_lidar_radar_resonance_kernel(
             w2_raw[:].bitcast(U16).rearrange("p a (m t) -> p a t m", t=PACK),
         )
         gather_words(1, 1)
+        w3_codes = keep.tile([P, N], U32, name="w3_codes", align_bytes=64)
+        for i0 in range(0, TILES, TILES // 2):
+            nc.vector.tensor_copy(
+                w3_codes[:].bitcast(I32).rearrange("p (i m) -> p m i", i=TILES)[:, :, i0 : i0 + TILES // 2],
+                w3_raw[:].bitcast(I32).rearrange("p (m i) -> p m i", i=TILES)[:, :, i0 : i0 + TILES // 2],
+            )
 
         h_all = [keep.tile([P, PACK, HALF], F32, name=f"h{s}") for s in range(HALVES)]
         y_all = [keep.tile([P, TILES, HALF], F32, name=f"y{s}") for s in range(HALVES)]
-        out_0_rows = out_0.rearrange("(i p) j -> p i j", p=P)
+        out_0_rows = out_0.rearrange("(p i) j -> p i j", i=TILES)
         h_codes = keep.tile([P, S], U32, name="h_codes", align_bytes=64)
         h_plane = keep.tile([P, S], U8, name="h_plane", align_bytes=64)
         out_1_rows = out_1.rearrange("(p t) j -> p t j", t=PACK)
@@ -250,7 +257,7 @@ def tile_list_lidar_radar_resonance_kernel(
                 )
 
         def keep_above(s, i):
-            nc.vector.tensor_tensor(y_all[s][:, i, :], match[s, i][:], floor[i // 2][:, i % 2, cols(s)], ALU.max)
+            nc.vector.tensor_tensor(y_all[s][:, i, :], match[s, i][:], floor[:, i, cols(s)], ALU.max)
             for i0, i1 in Y_STORES[s]:
                 if i1 == i + 1:
                     nc.sync.dma_start(out_0_rows[:, i0:i1, cols(s)], y_all[s][:, i0:i1, :])

@@ -28,6 +28,8 @@ QUARTER_ORDER = ((0, 1), (1, 0))
 Y_STORES = (((0, 2), (2, 4), (4, 6)), ((0, 2), (2, 3), (3, 4), (4, 5), (5, 6)))
 SLICE_PAIRS = ((0, 1), (2, 3))
 ROW_STEP = 4
+EARLY, LATE = 1, 0
+H_ROW = 4
 ROW = S + PASSES * H + N
 
 
@@ -46,8 +48,8 @@ def tile_list_lidar_radar_resonance_kernel(
         tab_rows = keep.tile([P, T], U8, name="tab_rows", align_bytes=64)
         w2_rows = keep.tile([P, PASSES * H + N], U8, name="w2_rows", align_bytes=64)
         rows = keep.tile([P, ROW], U8, name="rows", align_bytes=64)
-        widths = (S, ROW)
-        planes = [keep.tile([P, widths[a]], U8, name=f"planes{a}", align_bytes=64) for a in range(PASSES)]
+        early_plane = keep.tile([P, S], U8, name="early_plane", align_bytes=64)
+        planes = {EARLY: early_plane, LATE: rows}
         one = keep.tile([P, 1], F32, name="one")
         warm = keep.tile([P, 1], F32, name="warm")
         centre = keep.tile([P, PACK], F32, name="centre")
@@ -55,8 +57,7 @@ def tile_list_lidar_radar_resonance_kernel(
         nc.vector.memset(tab_rows[:].bitcast(I32), 0)
         nc.vector.memset(w2_rows[:].bitcast(I32), 0)
         nc.vector.memset(one[:], 1.0)
-        for a in range(PASSES):
-            nc.vector.memset(planes[a][:].bitcast(I32), 0)
+        nc.vector.memset(early_plane[:].bitcast(I32), 0)
         nc.scalar.activation(warm[:], one[:], ACT.Abs_reciprocal_sqrt)
 
         w1_codes = [keep.tile([P, H], U32, name=f"w1_codes{a}", align_bytes=64) for a in range(PASSES)]
@@ -86,21 +87,21 @@ def tile_list_lidar_radar_resonance_kernel(
             )
 
         nc.sync.dma_start(offsets[:], offs)
-        load_w1(1)
+        load_w1(LATE)
         nc.sync.dma_start(centre[:], centres.rearrange("(p t) -> p t", t=PACK))
         nc.sync.dma_start(
             tab_rows[0:P:ROW_STEP, :].bitcast(I32),
             tab_scales.bitcast(I32).rearrange("a q t -> q a t"),
         )
-        last_pass_rows = slice(ROW_STEP, P, PASSES * ROW_STEP)
+        last_pass_rows = slice(0, P, PASSES * ROW_STEP)
         nc.sync.dma_start(
             w2_rows[last_pass_rows, 0 : PASSES * H].bitcast(I32).rearrange("q (a c) -> q a c", a=PASSES),
             w2_scales.bitcast(I32).rearrange("a q c -> q a c"),
         )
         nc.sync.dma_start(w2_rows[last_pass_rows, PASSES * H :].bitcast(I32), w3_scales[0].bitcast(I32))
-        tab[0] = relay.tile([P, T], U32, name="tab0", offset=0, align_bytes=64)
-        load_tab(0)
-        load_w1(0)
+        tab[EARLY] = relay.tile([P, T], U32, name="tab_early", offset=0, align_bytes=64)
+        load_tab(EARLY)
+        load_w1(EARLY)
 
         v_rows = keep.tile([P, S], U8, name="v_rows", align_bytes=64)
         nc.vector.tensor_copy(v_rows[:], tab_rows[:].indirect(offsets[:]))
@@ -114,23 +115,23 @@ def tile_list_lidar_radar_resonance_kernel(
             w2_rows[:, PASSES * H :].rearrange("p (m i) -> p i m", i=TILES),
         )
 
-        def move_rows(a):
-            for r in range(4):
+        def move_rows(a, first, width):
+            for r in range(first, 4):
                 nc.sync.dma_start(
                     planes[a][r:P:32, :].bitcast(I32),
-                    rows[ROW_STEP * (PASSES * r + a) : P : 32, 0 : widths[a]].bitcast(I32),
+                    rows[ROW_STEP * (PASSES * r + a) : P : 32, 0:width].bitcast(I32),
                 )
 
-        move_rows(0)
-        tab[1] = keep.tile([P, T], U32, name="tab1", tag="v_rows", align_bytes=64)
-        load_tab(1)
-        move_rows(1)
+        move_rows(EARLY, 0, S)
+        tab[LATE] = keep.tile([P, T], U32, name="tab_late", tag="v_rows", align_bytes=64)
+        load_tab(LATE)
+        move_rows(LATE, 1, ROW)
 
         w2_codes = keep.tile([P, PASSES, 2 * H], U8, name="w2_codes", align_bytes=64)
-        quantise_w1(1)
-        gather_words(0, 0)
-        gather_words(0, 1)
-        quantise_w1(0)
+        quantise_w1(LATE)
+        gather_words(EARLY, 0)
+        gather_words(EARLY, 1)
+        quantise_w1(EARLY)
 
         w2_raw = relay.tile([P, PASSES, 2 * H], U8, name="w2_raw", offset=0, align_bytes=64)
         nc.sync.dma_start(w2_raw[:].bitcast(I32), w2_words.rearrange("a p b -> p a b").bitcast(I32))
@@ -139,12 +140,12 @@ def tile_list_lidar_radar_resonance_kernel(
         floor = relay.tile([P, TILES, S], F32, name="floor", offset=4 * H + 4 * N, align_bytes=64)
         nc.sync.dma_start(floor[:], least.rearrange("(p i) j -> p i j", i=TILES))
 
-        gather_words(1, 0)
+        gather_words(LATE, 0)
         nc.vector.tensor_copy(
             w2_codes[:].bitcast(U16).rearrange("p a (t m) -> p a t m", t=PACK),
             w2_raw[:].bitcast(U16).rearrange("p a (m t) -> p a t m", t=PACK),
         )
-        gather_words(1, 1)
+        gather_words(LATE, 1)
         w3_codes = keep.tile([P, N], U32, name="w3_codes", align_bytes=64)
         for i0 in range(0, TILES, TILES // 2):
             nc.vector.tensor_copy(
@@ -178,29 +179,29 @@ def tile_list_lidar_radar_resonance_kernel(
                 lhsT_scale=w1_plane[a][:, P * t : P * (t + 1)],
                 rhs=v_codes[a, s][:].bitcast(E4M3),
                 rhs_scale=planes[a][:, cols(s)],
-                start=(a == 0),
-                stop=(a == PASSES - 1),
+                start=(a == EARLY),
+                stop=(a == LATE),
             )
 
         def amp_pass(a, s, t):
             nc.tensor.matmul_mx(
                 amp[s, t][:],
                 lhsT=w2_codes[:, a, 2 * P * t : 2 * P * (t + 1)].bitcast(E2M1),
-                lhsT_scale=planes[1][:, S + H * a + P * t : S + H * a + P * (t + 1)],
+                lhsT_scale=rows[:, S + H * a + P * t : S + H * a + P * (t + 1)],
                 rhs=v_codes[a, s][:].bitcast(E4M3),
                 rhs_scale=planes[a][:, cols(s)],
-                start=(a == 0),
-                stop=(a == PASSES - 1),
+                start=(a == EARLY),
+                stop=(a == LATE),
             )
 
         def positions(s, t):
             pos[s, t] = psum.tile([P, HALF], F32, name=f"front{t}")
-            for a in range(PASSES):
+            for a in (EARLY, LATE):
                 pos_pass(a, s, t)
 
         def amplitudes(s, t):
             amp[s, t] = psum.tile([P, HALF], F32, name=f"amp{t}")
-            for a in range(PASSES):
+            for a in (EARLY, LATE):
                 amp_pass(a, s, t)
 
         def squared_gap(s, t):
@@ -232,13 +233,13 @@ def tile_list_lidar_radar_resonance_kernel(
 
         def quantise(s, e):
             c0 = s * HALF + e * QUARTER
-            nc.vector.quantize_mx(h_codes[:, c0 : c0 + QUARTER].bitcast(E4M3), h_plane[:, c0 : c0 + QUARTER], h_bf[s, e][:])
+            nc.vector.quantize_mx(h_codes[:, c0 : c0 + QUARTER].bitcast(E4M3), h_plane[H_ROW:P, c0 : c0 + QUARTER], h_bf[s, e][:])
 
         def store_codes(s):
             nc.sync.dma_start(out_2_words[:, cols(s)], h_codes[:, cols(s)].bitcast(I32))
             if s == HALVES - 1:
                 for r in range(4):
-                    nc.scalar.dma_start(out_3[0, r:16:4, :].bitcast(I32), h_plane[r:P:32, :].bitcast(I32))
+                    nc.scalar.dma_start(out_3[0, r:16:4, :].bitcast(I32), h_plane[H_ROW + r : P : 32, :].bitcast(I32))
 
         def score(s, i, bank):
             match[s, i] = psum.tile([P, HALF], F32, name=bank)
@@ -249,9 +250,9 @@ def tile_list_lidar_radar_resonance_kernel(
                 nc.tensor.matmul_mx(
                     match[s, i][:, e * QUARTER : (e + 1) * QUARTER],
                     lhsT=w3_codes[:, n0 : n0 + P].bitcast(E4M3),
-                    lhsT_scale=planes[1][:, plane0 : plane0 + P],
+                    lhsT_scale=rows[:, plane0 : plane0 + P],
                     rhs=h_codes[:, c0 : c0 + QUARTER].bitcast(E4M3),
-                    rhs_scale=h_plane[:, c0 : c0 + QUARTER],
+                    rhs_scale=h_plane[H_ROW:P, c0 : c0 + QUARTER],
                     start=True,
                     stop=True,
                 )
@@ -264,7 +265,7 @@ def tile_list_lidar_radar_resonance_kernel(
 
         for t in range(PACK):
             pos[0, t] = psum.tile([P, HALF], F32, name=f"front{t}")
-        for a in range(PASSES):
+        for a in (EARLY, LATE):
             for t in range(PACK):
                 pos_pass(a, 0, t)
         for t in range(PACK):

@@ -72,9 +72,9 @@ def tile_list_lidar_radar_resonance_kernel(
         def load_tab(a):
             nc.sync.dma_start(tab[a][:].bitcast(I32), tab_words[a].rearrange("p t i -> p (t i)").bitcast(I32))
 
-        def quantise_w1(a):
+        def quantise_w1(a, copy):
             w1_bf = keep.tile([P, PACK * H], BF16, name=f"w1_bf{a}", align_bytes=64)
-            nc.scalar.copy(
+            copy(
                 w1_bf[:].rearrange("p (t m j) -> p m t j", t=PACK, j=PACK),
                 w1_raw[a][:].rearrange("p j (m t) -> p m t j", t=PACK),
             )
@@ -110,10 +110,7 @@ def tile_list_lidar_radar_resonance_kernel(
             rows[:, S : S + PASSES * H].rearrange("p (a t m) -> p a t m", a=PASSES, t=PACK),
             w2_rows[:, 0 : PASSES * H].rearrange("p (a m t) -> p a t m", a=PASSES, t=PACK),
         )
-        nc.vector.tensor_copy(
-            rows[:, S + PASSES * H : ROW].rearrange("p (i m) -> p i m", i=TILES),
-            w2_rows[:, PASSES * H :].rearrange("p (m i) -> p i m", i=TILES),
-        )
+        nc.vector.tensor_copy(rows[:, S + PASSES * H : ROW].bitcast(I32), w2_rows[:, PASSES * H :].bitcast(I32))
 
         def move_rows(a, first, width):
             for r in range(first, 4):
@@ -128,34 +125,29 @@ def tile_list_lidar_radar_resonance_kernel(
         move_rows(LATE, 1, ROW)
 
         w2_codes = keep.tile([P, PASSES, 2 * H], U8, name="w2_codes", align_bytes=64)
-        quantise_w1(LATE)
+        quantise_w1(LATE, nc.scalar.copy)
         gather_words(EARLY, 0)
         gather_words(EARLY, 1)
-        quantise_w1(EARLY)
+        quantise_w1(EARLY, nc.vector.tensor_copy)
 
         w2_raw = relay.tile([P, PASSES, 2 * H], U8, name="w2_raw", offset=0, align_bytes=64)
         nc.sync.dma_start(w2_raw[:].bitcast(I32), w2_words.rearrange("a p b -> p a b").bitcast(I32))
-        w3_raw = relay.tile([P, N], U32, name="w3_raw", offset=4 * H, align_bytes=64)
-        nc.sync.dma_start(w3_raw[:].bitcast(I32), w3_words[0].rearrange("p c i -> p (c i)").bitcast(I32))
+        w3_codes = relay.tile([P, N], U32, name="w3_codes", offset=4 * H, align_bytes=64)
+        nc.sync.dma_start(w3_codes[:].bitcast(I32), w3_words[0].rearrange("p c i -> p (c i)").bitcast(I32))
         floor = relay.tile([P, TILES, S], F32, name="floor", offset=4 * H + 4 * N, align_bytes=64)
-        nc.sync.dma_start(floor[:], least.rearrange("(p i) j -> p i j", i=TILES))
+        nc.sync.dma_start(floor[:], least.rearrange("(i p) j -> p i j", p=P))
 
         gather_words(LATE, 0)
-        nc.vector.tensor_copy(
-            w2_codes[:].bitcast(U16).rearrange("p a (t m) -> p a t m", t=PACK),
-            w2_raw[:].bitcast(U16).rearrange("p a (m t) -> p a t m", t=PACK),
-        )
         gather_words(LATE, 1)
-        w3_codes = keep.tile([P, N], U32, name="w3_codes", align_bytes=64)
-        for i0 in range(0, TILES, TILES // 2):
+        for t0, t1 in SLICE_PAIRS:
             nc.vector.tensor_copy(
-                w3_codes[:].bitcast(I32).rearrange("p (i m) -> p m i", i=TILES)[:, :, i0 : i0 + TILES // 2],
-                w3_raw[:].bitcast(I32).rearrange("p (m i) -> p m i", i=TILES)[:, :, i0 : i0 + TILES // 2],
+                w2_codes[:].bitcast(U16).rearrange("p a (t m) -> p a t m", t=PACK)[:, :, t0 : t1 + 1, :],
+                w2_raw[:].bitcast(U16).rearrange("p a (m t) -> p a t m", t=PACK)[:, :, t0 : t1 + 1, :],
             )
 
         h_all = [keep.tile([P, PACK, HALF], F32, name=f"h{s}") for s in range(HALVES)]
         y_all = [keep.tile([P, TILES, HALF], F32, name=f"y{s}") for s in range(HALVES)]
-        out_0_rows = out_0.rearrange("(p i) j -> p i j", i=TILES)
+        out_0_rows = out_0.rearrange("(i p) j -> p i j", p=P)
         h_codes = keep.tile([P, S], U32, name="h_codes", align_bytes=64)
         h_plane = keep.tile([P, S], U8, name="h_plane", align_bytes=64)
         out_1_rows = out_1.rearrange("(p t) j -> p t j", t=PACK)

@@ -24,6 +24,7 @@ HALVES = S // HALF
 QUARTER = HALF // 2
 TILES = N // P
 FILL = 3
+W1_SPLIT = 88
 QUARTER_ORDER = ((0, 1), (1, 0))
 Y_STORES = (((0, 2), (2, 4), (4, 6)), ((0, 2), (2, 3), (3, 4), (4, 5), (5, 6)))
 SLICE_PAIRS = ((0, 1), (2, 3))
@@ -72,12 +73,13 @@ def tile_list_lidar_radar_resonance_kernel(
         def load_tab(a):
             nc.sync.dma_start(tab[a][:].bitcast(I32), tab_words[a].rearrange("p t i -> p (t i)").bitcast(I32))
 
-        def quantise_w1(a, copy):
+        def quantise_w1(a, shares):
             w1_bf = keep.tile([P, PACK * H], BF16, name=f"w1_bf{a}", align_bytes=64)
-            copy(
-                w1_bf[:].rearrange("p (t m j) -> p m t j", t=PACK, j=PACK),
-                w1_raw[a][:].rearrange("p j (m t) -> p m t j", t=PACK),
-            )
+            for copy, m0, m1 in shares:
+                copy(
+                    w1_bf[:].rearrange("p (t m j) -> p m t j", t=PACK, j=PACK)[:, m0:m1],
+                    w1_raw[a][:].rearrange("p j (m t) -> p m t j", t=PACK)[:, m0:m1],
+                )
             nc.vector.quantize_mx(w1_codes[a][:].bitcast(E4M3), w1_plane[a][:], w1_bf[:])
 
         def gather_words(a, s):
@@ -125,10 +127,10 @@ def tile_list_lidar_radar_resonance_kernel(
         move_rows(LATE, 1, ROW)
 
         w2_codes = keep.tile([P, PASSES, 2 * H], U8, name="w2_codes", align_bytes=64)
-        quantise_w1(LATE, nc.scalar.copy)
+        quantise_w1(LATE, ((nc.scalar.copy, 0, P),))
         gather_words(EARLY, 0)
         gather_words(EARLY, 1)
-        quantise_w1(EARLY, nc.vector.tensor_copy)
+        quantise_w1(EARLY, ((nc.vector.tensor_copy, 0, W1_SPLIT), (nc.scalar.copy, W1_SPLIT, P)))
 
         w2_raw = relay.tile([P, PASSES, 2 * H], U8, name="w2_raw", offset=0, align_bytes=64)
         nc.sync.dma_start(w2_raw[:].bitcast(I32), w2_words.rearrange("a p b -> p a b").bitcast(I32))
@@ -186,13 +188,11 @@ def tile_list_lidar_radar_resonance_kernel(
                 stop=(a == LATE),
             )
 
-        def positions(s, t):
-            pos[s, t] = psum.tile([P, HALF], F32, name=f"front{t}")
-            for a in (EARLY, LATE):
-                pos_pass(a, s, t)
+        def bank(b):
+            return psum.tile([P, HALF], F32, name=f"bank{b}")
 
         def amplitudes(s, t):
-            amp[s, t] = psum.tile([P, HALF], F32, name=f"amp{t}")
+            amp[s, t] = bank(t)
             for a in (EARLY, LATE):
                 amp_pass(a, s, t)
 
@@ -233,8 +233,8 @@ def tile_list_lidar_radar_resonance_kernel(
                 for r in range(4):
                     nc.scalar.dma_start(out_3[0, r:16:4, :].bitcast(I32), h_plane[H_ROW + r : P : 32, :].bitcast(I32))
 
-        def score(s, i, bank):
-            match[s, i] = psum.tile([P, HALF], F32, name=bank)
+        def score(s, i, b):
+            match[s, i] = bank(b)
             n0 = P * i
             plane0 = S + PASSES * H + n0
             for e in QUARTER_ORDER[s]:
@@ -255,19 +255,17 @@ def tile_list_lidar_radar_resonance_kernel(
                 if i1 == i + 1:
                     nc.sync.dma_start(out_0_rows[:, i0:i1, cols(s)], y_all[s][:, i0:i1, :])
 
-        for t in range(PACK):
-            pos[0, t] = psum.tile([P, HALF], F32, name=f"front{t}")
-        for a in (EARLY, LATE):
+        for s in range(HALVES):
             for t in range(PACK):
-                pos_pass(a, 0, t)
-        for t in range(PACK):
-            amplitudes(0, t)
+                pos[s, t] = bank(PACK * s + t)
+        for a in (EARLY, LATE):
+            for s in range(HALVES):
+                for t in range(PACK):
+                    pos_pass(a, s, t)
         for pair in SLICE_PAIRS:
-            for step in (squared_gap, inverse_root, response, amplify):
+            for step in (squared_gap, amplitudes, inverse_root, response, amplify):
                 for t in pair:
                     step(0, t)
-            for t in pair:
-                positions(1, t)
             for t in pair:
                 amplitudes(1, t)
         for e in range(2):
@@ -282,14 +280,14 @@ def tile_list_lidar_radar_resonance_kernel(
         round_h(1, 0, nc.scalar.copy)
         round_h(1, 1, nc.vector.tensor_copy)
         for i in range(TILES - FILL):
-            score(0, i, f"front{i % 3}")
+            score(0, i, PACK + i)
             keep_above(0, i)
         quantise(1, 1)
         quantise(1, 0)
         store_codes(1)
         for i in range(TILES - FILL, TILES):
-            score(0, i, f"amp{i - TILES + PACK}")
+            score(0, i, i - TILES + PACK)
             keep_above(0, i)
         for i in range(TILES):
-            score(1, i, f"front{i % PACK}")
+            score(1, i, PACK + i % PACK)
             keep_above(1, i)

from contextlib import ExitStack

import concourse.mybir as mybir

K, T, S, H, N = 1024, 4096, 1024, 512, 768
FLOPS = 2 * (2 * K * H * S + H * N * S)

F32 = mybir.dt.float32
BF16 = mybir.dt.bfloat16
I32 = mybir.dt.int32
U32 = mybir.dt.uint32
U16 = mybir.dt.uint16
U8 = mybir.dt.uint8
E4M3 = mybir.dt.float8_e4m3fn_x4
E2M1 = mybir.dt.float4_e2m1fn_x4
ACT = mybir.ActivationFunctionType
ALU = mybir.AluOpType

P = 128
PACK = 4
PASSES = K // (P * PACK)
HALF = 512
HALVES = S // HALF
QUARTER = HALF // 2
TILES = N // P
FILL = 3
W1_SPLIT = 88
QUARTER_ORDER = ((0, 1), (1, 0))
Y_STORES = (((0, 2), (2, 4), (4, 6)), ((0, 2), (2, 3), (3, 4), (4, 5), (5, 6)))
SLICE_PAIRS = ((0, 1), (2, 3))
ROW_STEP = 4
EARLY, LATE = 1, 0
H_ROW = 4
ROW = S + PASSES * H + N


def tile_list_lidar_radar_resonance_kernel(
    tc, tab_words, tab_scales, offs, w1, w2_words, w2_scales, w3_words, w3_scales, centres, least,
    out_0, out_1, out_2, out_3,
):
    nc = tc.nc
    with ExitStack() as ctx:
        keep = ctx.enter_context(tc.tile_pool(name="keep", bufs=1))
        work = ctx.enter_context(tc.tile_pool(name="work", bufs=2))
        relay = ctx.enter_context(tc.tile_pool(name="relay", bufs=1))
        psum = ctx.enter_context(tc.psum_pool(name="psum", bufs=1))

        offsets = keep.tile([P, S // 16], U16, name="offsets")
        tab_rows = keep.tile([P, T], U8, name="tab_rows", align_bytes=64)
        w2_rows = keep.tile([P, PASSES * H + N], U8, name="w2_rows", align_bytes=64)
        rows = keep.tile([P, ROW], U8, name="rows", align_bytes=64)
        early_plane = keep.tile([P, S], U8, name="early_plane", align_bytes=64)
        planes = {EARLY: early_plane, LATE: rows}
        one = keep.tile([P, 1], F32, name="one")
        warm = keep.tile([P, 1], F32, name="warm")
        centre = keep.tile([P, PACK], F32, name="centre")

        nc.vector.memset(tab_rows[:].bitcast(I32), 0)
        nc.vector.memset(w2_rows[:].bitcast(I32), 0)
        nc.vector.memset(one[:], 1.0)
        nc.vector.memset(early_plane[:].bitcast(I32), 0)
        nc.scalar.activation(warm[:], one[:], ACT.Abs_reciprocal_sqrt)

        w1_codes = [keep.tile([P, H], U32, name=f"w1_codes{a}", align_bytes=64) for a in range(PASSES)]
        w1_plane = [keep.tile([P, H], U8, name=f"w1_plane{a}", align_bytes=64) for a in range(PASSES)]
        w1_raw = [keep.tile([P, PACK, H], F32, name=f"w1_raw{a}") for a in range(PASSES)]
        tab = {}
        v_codes = {}

        def load_w1(a):
            nc.sync.dma_start(w1_raw[a][:], w1[512 * a : 512 * (a + 1), :].rearrange("(p j) c -> p j c", j=PACK))

        def load_tab(a):
            nc.sync.dma_start(tab[a][:].bitcast(I32), tab_words[a].rearrange("p t i -> p (t i)").bitcast(I32))

        def quantise_w1(a, shares):
            w1_bf = keep.tile([P, PACK * H], BF16, name=f"w1_bf{a}", align_bytes=64)
            for copy, m0, m1 in shares:
                copy(
                    w1_bf[:].rearrange("p (t m j) -> p m t j", t=PACK, j=PACK)[:, m0:m1],
                    w1_raw[a][:].rearrange("p j (m t) -> p m t j", t=PACK)[:, m0:m1],
                )
            nc.vector.quantize_mx(w1_codes[a][:].bitcast(E4M3), w1_plane[a][:], w1_bf[:])

        def gather_words(a, s):
            v_codes[a, s] = keep.tile([P, HALF], U32, name=f"v_codes{a}_{s}", align_bytes=64)
            nc.vector.tensor_copy(
                v_codes[a, s][:], tab[a][:].indirect(offsets[:, s * HALF // 16 : (s + 1) * HALF // 16])
            )

        nc.sync.dma_start(offsets[:], offs)
        load_w1(LATE)
        nc.sync.dma_start(centre[:], centres.rearrange("(p t) -> p t", t=PACK))
        nc.sync.dma_start(
            tab_rows[0:P:ROW_STEP, :].bitcast(I32),
            tab_scales.bitcast(I32).rearrange("a q t -> q a t"),
        )
        last_pass_rows = slice(0, P, PASSES * ROW_STEP)
        nc.sync.dma_start(
            w2_rows[last_pass_rows, 0 : PASSES * H].bitcast(I32).rearrange("q (a c) -> q a c", a=PASSES),
            w2_scales.bitcast(I32).rearrange("a q c -> q a c"),
        )
        nc.sync.dma_start(w2_rows[last_pass_rows, PASSES * H :].bitcast(I32), w3_scales[0].bitcast(I32))
        tab[EARLY] = relay.tile([P, T], U32, name="tab_early", offset=0, align_bytes=64)
        load_tab(EARLY)
        load_w1(EARLY)

        v_rows = keep.tile([P, S], U8, name="v_rows", align_bytes=64)
        nc.vector.tensor_copy(v_rows[:], tab_rows[:].indirect(offsets[:]))
        nc.vector.tensor_copy(rows[:, 0:S].bitcast(I32), v_rows[:].bitcast(I32))
        nc.vector.tensor_copy(
            rows[:, S : S + PASSES * H].rearrange("p (a t m) -> p a t m", a=PASSES, t=PACK),
            w2_rows[:, 0 : PASSES * H].rearrange("p (a m t) -> p a t m", a=PASSES, t=PACK),
        )
        nc.vector.tensor_copy(rows[:, S + PASSES * H : ROW].bitcast(I32), w2_rows[:, PASSES * H :].bitcast(I32))

        def move_rows(a, first, width):
            for r in range(first, 4):
                nc.sync.dma_start(
                    planes[a][r:P:32, :].bitcast(I32),
                    rows[ROW_STEP * (PASSES * r + a) : P : 32, 0:width].bitcast(I32),
                )

        move_rows(EARLY, 0, S)
        tab[LATE] = keep.tile([P, T], U32, name="tab_late", tag="v_rows", align_bytes=64)
        load_tab(LATE)
        move_rows(LATE, 1, ROW)

        w2_codes = keep.tile([P, PASSES, 2 * H], U8, name="w2_codes", align_bytes=64)
        quantise_w1(LATE, ((nc.scalar.copy, 0, P),))
        gather_words(EARLY, 0)
        gather_words(EARLY, 1)
        quantise_w1(EARLY, ((nc.vector.tensor_copy, 0, W1_SPLIT), (nc.scalar.copy, W1_SPLIT, P)))

        w2_raw = relay.tile([P, PASSES, 2 * H], U8, name="w2_raw", offset=0, align_bytes=64)
        nc.sync.dma_start(w2_raw[:].bitcast(I32), w2_words.rearrange("a p b -> p a b").bitcast(I32))
        w3_codes = relay.tile([P, N], U32, name="w3_codes", offset=4 * H, align_bytes=64)
        nc.sync.dma_start(w3_codes[:].bitcast(I32), w3_words[0].rearrange("p c i -> p (c i)").bitcast(I32))
        floor = relay.tile([P, TILES, S], F32, name="floor", offset=4 * H + 4 * N, align_bytes=64)
        nc.sync.dma_start(floor[:], least.rearrange("(i p) j -> p i j", p=P))

        gather_words(LATE, 0)
        gather_words(LATE, 1)
        for t0, t1 in SLICE_PAIRS:
            nc.vector.tensor_copy(
                w2_codes[:].bitcast(U16).rearrange("p a (t m) -> p a t m", t=PACK)[:, :, t0 : t1 + 1, :],
                w2_raw[:].bitcast(U16).rearrange("p a (m t) -> p a t m", t=PACK)[:, :, t0 : t1 + 1, :],
            )

        h_all = [keep.tile([P, PACK, HALF], F32, name=f"h{s}") for s in range(HALVES)]
        y_all = [keep.tile([P, TILES, HALF], F32, name=f"y{s}") for s in range(HALVES)]
        out_0_rows = out_0.rearrange("(i p) j -> p i j", p=P)
        h_codes = keep.tile([P, S], U32, name="h_codes", align_bytes=64)
        h_plane = keep.tile([P, S], U8, name="h_plane", align_bytes=64)
        out_1_rows = out_1.rearrange("(p t) j -> p t j", t=PACK)
        out_2_words = out_2[0].rearrange("p m t -> p (m t)").bitcast(I32)

        pos = {}
        amp = {}
        square = {}
        root = {}
        resp = {}
        h_bf = {}
        match = {}

        def cols(s):
            return slice(s * HALF, (s + 1) * HALF)

        def pos_pass(a, s, t):
            nc.tensor.matmul_mx(
                pos[s, t][:],
                lhsT=w1_codes[a][:, P * t : P * (t + 1)].bitcast(E4M3),
                lhsT_scale=w1_plane[a][:, P * t : P * (t + 1)],
                rhs=v_codes[a, s][:].bitcast(E4M3),
                rhs_scale=planes[a][:, cols(s)],
                start=(a == EARLY),
                stop=(a == LATE),
            )

        def amp_pass(a, s, t):
            nc.tensor.matmul_mx(
                amp[s, t][:],
                lhsT=w2_codes[:, a, 2 * P * t : 2 * P * (t + 1)].bitcast(E2M1),
                lhsT_scale=rows[:, S + H * a + P * t : S + H * a + P * (t + 1)],
                rhs=v_codes[a, s][:].bitcast(E4M3),
                rhs_scale=planes[a][:, cols(s)],
                start=(a == EARLY),
                stop=(a == LATE),
            )

        def bank(b):
            return psum.tile([P, HALF], F32, name=f"bank{b}")

        def amplitudes(s, t):
            amp[s, t] = bank(t)
            for a in (EARLY, LATE):
                amp_pass(a, s, t)

        def squared_gap(s, t):
            square[s, t] = work.tile([P, HALF], F32, name="square")
            nc.scalar.activation(square[s, t][:], pos[s, t][:], ACT.Square, bias=centre[:, t : t + 1], scale=-1.0)

        def inverse_root(s, t):
            root[s, t] = work.tile([P, HALF], F32, name="root", bufs=4)
            nc.scalar.activation(root[s, t][:], square[s, t][:], ACT.Abs_reciprocal_sqrt, bias=one[:])

        def response(s, t):
            resp[s, t] = work.tile([P, HALF], F32, name="resp", bufs=4)
            if s == 0:
                nc.vector.tensor_tensor(resp[s, t][:], root[s, t][:], root[s, t][:], ALU.mult)
            else:
                nc.scalar.activation(resp[s, t][:], root[s, t][:], ACT.Square)

        def amplify(s, t):
            nc.vector.tensor_tensor(h_all[s][:, t, :], amp[s, t][:], resp[s, t][:], ALU.mult)
            if t % 2 == 1:
                nc.sync.dma_start(out_1_rows[:, t - 1 : t + 1, cols(s)], h_all[s][:, t - 1 : t + 1, :])

        def round_h(s, e, copy):
            h_bf[s, e] = keep.tile([P, PACK * QUARTER], BF16, name=f"h_bf{s}_{e}", align_bytes=64)
            copy(
                h_bf[s, e][:].rearrange("p (c i t) -> p c t i", t=PACK, i=4),
                h_all[s][:, :, e * QUARTER : (e + 1) * QUARTER].rearrange("p t (c i) -> p c t i", i=4),
            )

        def quantise(s, e):
            c0 = s * HALF + e * QUARTER
            nc.vector.quantize_mx(h_codes[:, c0 : c0 + QUARTER].bitcast(E4M3), h_plane[H_ROW:P, c0 : c0 + QUARTER], h_bf[s, e][:])

        def store_codes(s):
            nc.sync.dma_start(out_2_words[:, cols(s)], h_codes[:, cols(s)].bitcast(I32))
            if s == HALVES - 1:
                for r in range(4):
                    nc.scalar.dma_start(out_3[0, r:16:4, :].bitcast(I32), h_plane[H_ROW + r : P : 32, :].bitcast(I32))

        def score(s, i, b):
            match[s, i] = bank(b)
            n0 = P * i
            plane0 = S + PASSES * H + n0
            for e in QUARTER_ORDER[s]:
                c0 = s * HALF + e * QUARTER
                nc.tensor.matmul_mx(
                    match[s, i][:, e * QUARTER : (e + 1) * QUARTER],
                    lhsT=w3_codes[:, n0 : n0 + P].bitcast(E4M3),
                    lhsT_scale=rows[:, plane0 : plane0 + P],
                    rhs=h_codes[:, c0 : c0 + QUARTER].bitcast(E4M3),
                    rhs_scale=h_plane[H_ROW:P, c0 : c0 + QUARTER],
                    start=True,
                    stop=True,
                )

        def keep_above(s, i):
            nc.vector.tensor_tensor(y_all[s][:, i, :], match[s, i][:], floor[:, i, cols(s)], ALU.max)
            for i0, i1 in Y_STORES[s]:
                if i1 == i + 1:
                    nc.sync.dma_start(out_0_rows[:, i0:i1, cols(s)], y_all[s][:, i0:i1, :])

        for s in range(HALVES):
            for t in range(PACK):
                pos[s, t] = bank(PACK * s + t)
        for a in (EARLY, LATE):
            for s in range(HALVES):
                for t in range(PACK):
                    pos_pass(a, s, t)
        for pair in SLICE_PAIRS:
            for step in (squared_gap, amplitudes, inverse_root, response, amplify):
                for t in pair:
                    step(0, t)
            for t in pair:
                amplitudes(1, t)
        for e in range(2):
            round_h(0, e, nc.vector.tensor_copy)
        for e in range(2):
            quantise(0, e)
        store_codes(0)
        for pair in SLICE_PAIRS:
            for step in (squared_gap, inverse_root, response, amplify):
                for t in pair:
                    step(1, t)
        round_h(1, 0, nc.scalar.copy)
        round_h(1, 1, nc.vector.tensor_copy)
        for i in range(TILES - FILL):
            score(0, i, PACK + i)
            keep_above(0, i)
        quantise(1, 1)
        quantise(1, 0)
        store_codes(1)
        for i in range(TILES - FILL, TILES):
            score(0, i, i - TILES + PACK)
            keep_above(0, i)
        for i in range(TILES):
            score(1, i, PACK + i % PACK)
            keep_above(1, i)
